import numpy as np
import ml_dtypes


def mxq(x, axis, fmt="e4m3"):
    dtype, down = {"e4m3": (ml_dtypes.float8_e4m3fn, 7), "e5m2": (ml_dtypes.float8_e5m2, 14)}[fmt]
    v = np.moveaxis(np.asarray(x, np.float32).astype(ml_dtypes.bfloat16).astype(np.float64), axis, -1)
    blocks = v.reshape(v.shape[:-1] + (-1, 32))
    amax = np.abs(blocks).max(-1, keepdims=True)
    byte = np.maximum(np.where(amax > 0, np.frexp(amax)[1] - 1 + 127, 0) - down, 1)
    scale = np.exp2(byte - 127.0)
    codes = (blocks / scale).astype(np.float32).astype(dtype).astype(np.float64)
    return np.moveaxis((codes * scale).reshape(v.shape), -1, axis)


WIDE = False


def mx_kscale(k):
    if not WIDE:
        return np.ones(k)
    levels = np.array([10, -10, 5, -5, 0])
    if k % 512:
        return np.exp2(np.random.permutation(np.resize(levels, k // 32))).repeat(32)
    a = np.empty((k // 512, 16))
    for p in range(k // 512):
        a[p, :8] = np.random.permutation(np.resize(levels, 8))
        for g in range(8):
            far = levels[np.abs(levels - a[p, g]) >= 10]
            a[p, g + 8] = far[np.random.randint(len(far))]
    return np.exp2(a.ravel()).repeat(32)


def f64(x):
    return np.asarray(x).astype(np.float64)


def striped(idx):
    return np.tile(idx.reshape(-1, 16).T, (8, 1)).astype(np.uint16)


def unstriped(offs):
    return offs[:16].T.reshape(-1).astype(np.int64)


E2M1 = np.array([0.0, 0.5, 1.0, 1.5, 2.0, 3.0, 4.0, 6.0, -0.0, -0.5, -1.0, -1.5, -2.0, -3.0, -4.0, -6.0])


def pack_weight(w, fmt):
    k, n = w.shape
    w = f64(np.asarray(w, np.float32).astype(ml_dtypes.bfloat16)).reshape(k // 32, 32, n)
    amax = np.abs(w).max(1)
    if fmt == "e4m3":
        byte = np.frexp(amax)[1] - 1 + 127 - 7
    else:
        mant, ex = np.frexp(amax / 6.0)
        byte = np.where(mant > 0.5, ex, ex - 1) + 127
    byte = np.clip(np.where(amax > 0, byte, 1), 1, 254)
    scaled = (w * np.exp2(127.0 - byte)[:, None, :]).reshape(k, n).astype(np.float32)
    by_word = np.ascontiguousarray(scaled.reshape(k // 512, 128, 4, n).transpose(0, 1, 3, 2))
    if fmt == "e4m3":
        words = by_word.astype(ml_dtypes.float8_e4m3fn).view(np.uint8)
    else:
        c = by_word.astype(ml_dtypes.float4_e2m1fn).view(np.uint8) & 0xF
        words = (c[..., 0::2] | (c[..., 1::2] << 4)).reshape(k // 512, 128, 2 * n)
    return np.ascontiguousarray(words), np.ascontiguousarray(byte.astype(np.uint8).reshape(k // 512, 16, n))


def unpack_weight(words, scales, fmt):
    g, _, n = scales.shape
    words = np.ascontiguousarray(words).reshape(g, 128, n, -1)
    if fmt == "e4m3":
        vals = words.view(ml_dtypes.float8_e4m3fn).astype(np.float64)
    else:
        nib = np.empty((g, 128, n, 4), np.uint8)
        nib[..., 0::2] = words & 0xF
        nib[..., 1::2] = words >> 4
        vals = E2M1[nib]
    vals = vals * np.repeat(np.exp2(scales.astype(np.float64) - 127.0), 8, axis=1)[..., None]
    return vals.transpose(0, 1, 3, 2).reshape(g * 512, n)


K, T, E, C, N = 512, 768, 6, 256, 256


def by_expert(wq, xq):
    return np.concatenate([wq[e].T @ xq[:, e * C:(e + 1) * C] for e in range(E)], axis=1)


def setup_inputs():
    n = np.random.standard_normal
    s = mx_kscale(K)
    first = np.random.permutation(np.repeat(np.arange(E), T // E))
    second = (first + 1 + np.random.permutation(np.repeat(np.arange(E - 1), -(-T // (E - 1)))[:T])) % E
    while np.bincount(second, minlength=E).max() != T // E:
        load = np.bincount(second, minlength=E); hi, lo = int(load.argmax()), int(load.argmin())
        t = np.flatnonzero((second == hi) & (first != lo))[0]; second[t] = lo
    slot_token = np.empty(E * C, np.int64); pos = np.empty((2, T), np.int64); fill = np.zeros(E, np.int64)
    place = np.stack([np.random.permutation(C) for _ in range(E)])
    for r, deal in enumerate((first, second)):
        for t in np.random.permutation(T):
            e = deal[t]; j = e * C + place[e, fill[e]]; fill[e] += 1; slot_token[j] = t; pos[r, t] = j
    g = np.random.uniform(0.2, 0.8, T)
    x = pack_weight(n((K, T)) * s[:, None], "e4m3")
    wq = [pack_weight(m, "e2m1") for m in n((E, K, N)) / np.sqrt(K) / s[None, :, None]]
    wv = [pack_weight(m, "e2m1") for m in n((E, K, N)) / np.sqrt(K) / s[None, :, None]]
    return {
        "x_words": x[0],
        "x_scales": x[1],
        "wq_words": np.stack([m[0] for m in wq]),
        "wq_scales": np.stack([m[1] for m in wq]),
        "wk": (n((E, K, N)) / np.sqrt(K) / s[None, :, None]).astype(np.float32),
        "wv_words": np.stack([m[0] for m in wv]),
        "wv_scales": np.stack([m[1] for m in wv]),
        "bias": (0.3 * n((3 * N, E))).astype(np.float32),
        "gate": np.stack([np.tile(g, (128, 1)), np.tile(1.0 - g, (128, 1))]).astype(np.float32),
        "offs": striped(slot_token),
        "pos1": striped(pos[0]),
        "pos2": striped(pos[1]),
    }


def reference(x_words, x_scales, wq_words, wq_scales, wk, wv_words, wv_scales, bias, gate, offs, pos1, pos2):
    wq = np.stack([unpack_weight(wq_words[e], wq_scales[e], "e2m1") for e in range(E)])
    wkq = mxq(f64(wk), 1, "e4m3")
    wv = np.stack([unpack_weight(wv_words[e], wv_scales[e], "e2m1") for e in range(E)])
    idx = unstriped(offs)
    xq = unpack_weight(x_words, x_scales, "e4m3")[:, idx]
    y = np.concatenate([by_expert(w, xq) for w in (wq, wkq, wv)])
    y = y + np.repeat(f64(bias), C, axis=1)
    out = sum(f64(gate[r, :1]) * y[:, unstriped(p)] for r, p in enumerate((pos1, pos2)))
    return out

@@ -1,0 +1,182 @@
+from contextlib import ExitStack
+
+import concourse.mybir as mybir
+from concourse.masks import make_identity
+
+K, T, E, C, N = 512, 768, 6, 256, 256
+S = E * C
+FLOPS = 2 * K * S * 3 * N
+
+F32 = mybir.dt.float32
+BF16 = mybir.dt.bfloat16
+I32 = mybir.dt.int32
+U32 = mybir.dt.uint32
+U16 = mybir.dt.uint16
+U8 = mybir.dt.uint8
+FP8X4 = mybir.dt.float8_e4m3fn_x4
+FP4X4 = mybir.dt.float4_e2m1fn_x4
+MULT = mybir.AluOpType.mult
+ADD = mybir.AluOpType.add
+IDENT = mybir.ActivationFunctionType.Identity
+
+P = 128
+N_PE = 0
+HALF = T // 2
+TAIL_CUTS = (0, 512, 768)
+WORD_CUTS = (0, 512, 1024, 1536)
+BYTE_CUTS = (0, 512, 1024, 1280, 1536)
+VEC_CASTS = ()
+
+
+def tile_moe_qkv_kernel(
+    tc, x_words, x_scales, wq_words, wq_scales, wk, wv_words, wv_scales, bias, gate, offs, pos1, pos2, out
+):
+    nc = tc.nc
+    with ExitStack() as ctx:
+        keep = ctx.enter_context(tc.tile_pool(name="keep", bufs=1))
+        ring = ctx.enter_context(tc.tile_pool(name="ring", bufs=3))
+        ypsum = ctx.enter_context(tc.psum_pool(name="ypsum", bufs=4))
+        tpsum = ctx.enter_context(tc.psum_pool(name="tpsum", bufs=2))
+
+        offs_sb = keep.tile([P, S // 16], U16, name="offs_sb")
+        pos1_sb = keep.tile([P, T // 16], U16, name="pos1_sb")
+        pos2_sb = keep.tile([P, T // 16], U16, name="pos2_sb")
+        xw = keep.tile([P, T], I32, name="xw", align_bytes=64)
+        xs = keep.tile([P, T], U8, name="xs", align_bytes=64)
+        xw_g = keep.tile([P, S], U32, name="xw_g", align_bytes=64)
+        xs_g = keep.tile([P, S], U8, name="xs_g", align_bytes=64)
+        wq_w = keep.tile([P, E, 2 * N], U8, name="wq_w", align_bytes=64)
+        wv_w = keep.tile([P, E, 2 * N], U8, name="wv_w", align_bytes=64)
+        wq_s = keep.tile([P, E, N], U8, name="wq_s", align_bytes=64)
+        wv_s = keep.tile([P, E, N], U8, name="wv_s", align_bytes=64)
+        wk_raw = [keep.tile([P, 4, N], F32, name="wk_raw%d" % e) for e in range(E)]
+        wk_bf = [keep.tile([P, N, 4], BF16, name="wk_bf%d" % e, align_bytes=64) for e in range(E)]
+        wk_w = [keep.tile([P, N], U32, name="wk_w%d" % e, align_bytes=64) for e in range(E)]
+        wk_s = [keep.tile([P, N], U8, name="wk_s%d" % e, align_bytes=64) for e in range(E)]
+        bias_sb = keep.tile([P, 6, 8], F32, name="bias_sb")
+        g1 = keep.tile([P, T], F32, name="g1")
+        g2 = keep.tile([P, T], F32, name="g2")
+        y = [keep.tile([P, S], F32, name="y%d" % b) for b in range(6)]
+        ident = keep.tile([P, P], F32, name="ident")
+        warm = keep.tile([P, 8], F32, name="warm")
+
+        nc.vector.memset(xs[:].bitcast(I32), 0)
+        nc.vector.memset(warm[:, 0:1], 0.0)
+        nc.scalar.activation(warm[:, 4:5], warm[:, 0:1], IDENT)
+        nc.vector.memset(wq_s[:].rearrange("p e n -> p (e n)").bitcast(I32), 0)
+        nc.vector.memset(wv_s[:].rearrange("p e n -> p (e n)").bitcast(I32), 0)
+
+        def load_wk(e):
+            nc.sync.dma_start(wk_raw[e][:], wk[e].rearrange("(p j) n -> p j n", j=4))
+
+        def load_words(dst, src):
+            nc.sync.dma_start(dst[:].bitcast(I32), src.rearrange("e s p b -> p (e s) b").bitcast(I32))
+
+        def load_scales(dst, src):
+            for q in range(4):
+                nc.sync.dma_start(
+                    dst[32 * q : 32 * q + 4, :, :].bitcast(I32),
+                    src[:, 0, 4 * q : 4 * q + 4, :].rearrange("e i n -> i e n").bitcast(I32),
+                )
+
+        nc.sync.dma_start(offs_sb[:], offs)
+        nc.sync.dma_start(xw[:], x_words[0].rearrange("p t d -> p (t d)").bitcast(I32))
+        load_wk(0)
+        for q in range(4):
+            nc.sync.dma_start(xs[32 * q : 32 * q + 4, :].bitcast(I32), x_scales[0, 4 * q : 4 * q + 4, :].bitcast(I32))
+        load_words(wq_w, wq_words)
+        load_scales(wq_s, wq_scales)
+        nc.sync.dma_start(bias_sb[:, :, 0:E], bias.rearrange("(b p) e -> p b e", p=P))
+        load_wk(1)
+        nc.sync.dma_start(pos1_sb[:], pos1)
+        nc.sync.dma_start(g1[:], gate[0])
+        nc.sync.dma_start(pos2_sb[:], pos2)
+        nc.sync.dma_start(g2[:], gate[1])
+        load_words(wv_w, wv_words)
+        load_scales(wv_s, wv_scales)
+        for e in range(2, E):
+            load_wk(e)
+
+        for a, b in zip(WORD_CUTS[:-1], WORD_CUTS[1:]):
+            nc.vector.tensor_copy(xw_g[:, a:b], xw[:].bitcast(U32).indirect(offs_sb[:, a // 16 : b // 16]))
+        for a, b in zip(BYTE_CUTS[:-1], BYTE_CUTS[1:]):
+            nc.vector.tensor_copy(xs_g[:, a:b], xs[:].indirect(offs_sb[:, a // 16 : b // 16]))
+
+        def quantise_wk(e):
+            src = wk_raw[e][:].rearrange("p j n -> p n j")
+            if e in VEC_CASTS:
+                nc.vector.tensor_copy(wk_bf[e][:], src)
+            else:
+                for h in range(2):
+                    nc.scalar.copy(wk_bf[e][:, h * P : (h + 1) * P, :], src[:, h * P : (h + 1) * P, :])
+            nc.vector.quantize_mx(
+                out=wk_w[e][:].bitcast(FP8X4), scales=wk_s[e][:], in_=wk_bf[e][:].rearrange("p n j -> p (n j)")
+            )
+
+        def project(b):
+            which, m = divmod(b, 2)
+            for e in range(E):
+                if which == 1:
+                    w = wk_w[e][:, m * P : (m + 1) * P].bitcast(FP8X4)
+                    ws = wk_s[e][:, m * P : (m + 1) * P]
+                else:
+                    w = (wq_w, None, wv_w)[which][:, e, 2 * m * P : 2 * (m + 1) * P].bitcast(FP4X4)
+                    ws = (wq_s, None, wv_s)[which][:, e, m * P : (m + 1) * P]
+                acc = ypsum.tile([P, C], F32, name="acc")
+                nc.tensor.matmul_mx(
+                    out=acc[:],
+                    lhsT=w,
+                    lhsT_scale=ws,
+                    rhs=xw_g[:, e * C : (e + 1) * C].bitcast(FP8X4),
+                    rhs_scale=xs_g[:, e * C : (e + 1) * C],
+                    start=True,
+                    stop=True,
+                )
+                nc.scalar.activation(y[b][:, e * C : (e + 1) * C], acc[:], IDENT, bias=bias_sb[:, b, e : e + 1])
+
+        def combine_pe(b):
+            pa = ring.tile([P, T], F32, name="pa")
+            pb = ring.tile([P, T], F32, name="pb")
+            res = ring.tile([P, T], F32, name="res")
+            nc.vector.tensor_tensor(pa[:], y[b][:].indirect(pos1_sb[:]), g1[:], MULT)
+            nc.vector.tensor_tensor(pb[:], y[b][:].indirect(pos2_sb[:]), g2[:], MULT)
+            for h in range(2):
+                turned = tpsum.tile([P, HALF], F32, name="turned")
+                for c in range(HALF // P):
+                    t0 = h * HALF + c * P
+                    nc.tensor.matmul(turned[:, c * P : (c + 1) * P], lhsT=pa[:, t0 : t0 + P], rhs=ident[:], start=True, stop=False, is_transpose=True)
+                    nc.tensor.matmul(turned[:, c * P : (c + 1) * P], lhsT=pb[:, t0 : t0 + P], rhs=ident[:], start=False, stop=True, is_transpose=True)
+                summed = ring.tile([P, HALF], F32, name="summed")
+                nc.scalar.copy(summed[:], turned[:])
+                back = tpsum.tile([P, HALF], F32, name="back")
+                for c in range(HALF // P):
+                    nc.tensor.transpose(back[:, c * P : (c + 1) * P], summed[:, c * P : (c + 1) * P], ident[:])
+                nc.scalar.copy(res[:, h * HALF : (h + 1) * HALF], back[:])
+            nc.sync.dma_start(out[b * P : (b + 1) * P, :], res[:])
+
+        def combine_vec(b, cuts):
+            pa = ring.tile([P, T], F32, name="pa")
+            pb = ring.tile([P, T], F32, name="pb")
+            res = ring.tile([P, T], F32, name="res")
+            for t0, t1 in zip(cuts[:-1], cuts[1:]):
+                nc.vector.tensor_tensor(pa[:, t0:t1], y[b][:].indirect(pos1_sb[:, t0 // 16 : t1 // 16]), g1[:, t0:t1], MULT)
+                nc.vector.tensor_tensor(pb[:, t0:t1], y[b][:].indirect(pos2_sb[:, t0 // 16 : t1 // 16]), g2[:, t0:t1], MULT)
+                nc.vector.tensor_tensor(res[:, t0:t1], pa[:, t0:t1], pb[:, t0:t1], ADD)
+                nc.sync.dma_start(out[b * P : (b + 1) * P, t0:t1], res[:, t0:t1])
+
+        order = (0, 1, 4, 5, 2, 3)
+        quant_after = ((0, 1), (2, 3), (4, 5), (), (), ())
+        project(order[0])
+        for i, b in enumerate(order):
+            if i + 1 < 6 and i + 1 != 4:
+                project(order[i + 1])
+            for e in quant_after[i]:
+                quantise_wk(e)
+            if i + 1 == 4:
+                project(order[i + 1])
+            if i < N_PE:
+                combine_pe(b)
+            elif i < 5:
+                combine_vec(b, (0, T))
+            else:
+                combine_vec(b, TAIL_CUTS)

@@ -20,12 +20,13 @@ ADD = mybir.AluOpType.add
 IDENT = mybir.ActivationFunctionType.Identity
 
 P = 128
-N_PE = 0
-HALF = T // 2
-TAIL_CUTS = (0, 512, 768)
-WORD_CUTS = (0, 512, 1024, 1536)
-BYTE_CUTS = (0, 512, 1024, 1280, 1536)
-VEC_CASTS = ()
+XG = (('w',0,512),('w',512,1024),('w',1024,1536),('s',0,512),('s',512,1024),('s',1024,1280),('s',1280,1536))
+SEQ = [('c', 2), ('P', 0, 0), ('c', 1), ('P', 0, 1), ('c', 3), ('P', 1, 0), ('P', 1, 1), ('P', 5, 0), ('q', 1), ('A', 0), ('c', 0), ('P', 5, 1), ('q', 0), ('c', 4), ('B', 0), ('T1', 0, 0, 512), ('P', 4, 0), ('q', 2), ('c', 5), ('A', 1), ('P', 2, 0), ('B', 1), ('A', 5), ('q', 4), ('q', 5), ('T1', 1, 0, 512), ('P', 4, 1), ('A', 4), ('q', 3), ('B', 4), ('P', 2, 1), ('P', 3, 0), ('B', 5), ('T2', 0, 0, 512), ('T2', 1, 0, 512), ('A', 2), ('T1', 5, 0, 512), ('T1', 4, 0, 512), ('add', 5, 512), ('P', 3, 1), ('T2', 4, 0, 512), ('B', 2), ('T2', 5, 0, 512), ('add', 2, 512), ('add', 0, 512), ('T1', 2, 0, 512), ('st', 5), ('T2', 2, 0, 512), ('add', 1, 512), ('st', 1), ('add', 4, 512), ('tail1',), ('tail2',), ('st', 4), ('st', 2), ('st', 0)]
+DMA = ['xw', 'offs', 'xs', 'wk0', 'wv', 'wk1', 'wqs', 'wk2', 'pos2', 'wq', 'pos1', 'bias', 'wvs', 'g', 'wk3', 'wk5', 'wk4']
+AFTER_Q = {('A',0): 0, ('B',4): 5, ('B',1): 2, ('B',2): 3, ('A',2): 4}
+AFTER_C = {0: ('T2', 0), 5: ('T2', 4), 3: ('P', 4), 1: ('T1', 1, 0, 512), 4: ('T1', 4, 0, 512)}
+BANKS = 8
+TAIL = 512
 
 
 def tile_moe_qkv_kernel(
@@ -34,9 +35,8 @@ def tile_moe_qkv_kernel(
     nc = tc.nc
     with ExitStack() as ctx:
         keep = ctx.enter_context(tc.tile_pool(name="keep", bufs=1))
-        ring = ctx.enter_context(tc.tile_pool(name="ring", bufs=3))
-        ypsum = ctx.enter_context(tc.psum_pool(name="ypsum", bufs=4))
-        tpsum = ctx.enter_context(tc.psum_pool(name="tpsum", bufs=2))
+        work = ctx.enter_context(tc.tile_pool(name="work", bufs=1))
+        psum = ctx.enter_context(tc.psum_pool(name="psum", bufs=1))
 
         offs_sb = keep.tile([P, S // 16], U16, name="offs_sb")
         pos1_sb = keep.tile([P, T // 16], U16, name="pos1_sb")
@@ -49,14 +49,12 @@ def tile_moe_qkv_kernel(
         wv_w = keep.tile([P, E, 2 * N], U8, name="wv_w", align_bytes=64)
         wq_s = keep.tile([P, E, N], U8, name="wq_s", align_bytes=64)
         wv_s = keep.tile([P, E, N], U8, name="wv_s", align_bytes=64)
-        wk_raw = [keep.tile([P, 4, N], F32, name="wk_raw%d" % e) for e in range(E)]
-        wk_bf = [keep.tile([P, N, 4], BF16, name="wk_bf%d" % e, align_bytes=64) for e in range(E)]
+        wk_raw = [work.tile([P, 4, N], F32, name="wk_raw%d" % e, tag="raw%d" % e, align_bytes=64) for e in range(E)]
+        wk_bf = [work.tile([P, N, 4], BF16, name="wk_bf%d" % e, tag="bf%d" % e, align_bytes=64) for e in range(E)]
         wk_w = [keep.tile([P, N], U32, name="wk_w%d" % e, align_bytes=64) for e in range(E)]
         wk_s = [keep.tile([P, N], U8, name="wk_s%d" % e, align_bytes=64) for e in range(E)]
         bias_sb = keep.tile([P, 6, 8], F32, name="bias_sb")
-        g1 = keep.tile([P, T], F32, name="g1")
-        g2 = keep.tile([P, T], F32, name="g2")
-        y = [keep.tile([P, S], F32, name="y%d" % b) for b in range(6)]
+        g12 = keep.tile([P, 2, T], F32, name="g12")
         ident = keep.tile([P, P], F32, name="ident")
         warm = keep.tile([P, 8], F32, name="warm")
 
@@ -65,9 +63,7 @@ def tile_moe_qkv_kernel(
         nc.scalar.activation(warm[:, 4:5], warm[:, 0:1], IDENT)
         nc.vector.memset(wq_s[:].rearrange("p e n -> p (e n)").bitcast(I32), 0)
         nc.vector.memset(wv_s[:].rearrange("p e n -> p (e n)").bitcast(I32), 0)
-
-        def load_wk(e):
-            nc.sync.dma_start(wk_raw[e][:], wk[e].rearrange("(p j) n -> p j n", j=4))
+        make_identity(nc, ident[:])
 
         def load_words(dst, src):
             nc.sync.dma_start(dst[:].bitcast(I32), src.rearrange("e s p b -> p (e s) b").bitcast(I32))
@@ -79,104 +75,135 @@ def tile_moe_qkv_kernel(
                     src[:, 0, 4 * q : 4 * q + 4, :].rearrange("e i n -> i e n").bitcast(I32),
                 )
 
-        nc.sync.dma_start(offs_sb[:], offs)
-        nc.sync.dma_start(xw[:], x_words[0].rearrange("p t d -> p (t d)").bitcast(I32))
-        load_wk(0)
-        for q in range(4):
-            nc.sync.dma_start(xs[32 * q : 32 * q + 4, :].bitcast(I32), x_scales[0, 4 * q : 4 * q + 4, :].bitcast(I32))
-        load_words(wq_w, wq_words)
-        load_scales(wq_s, wq_scales)
-        nc.sync.dma_start(bias_sb[:, :, 0:E], bias.rearrange("(b p) e -> p b e", p=P))
-        load_wk(1)
-        nc.sync.dma_start(pos1_sb[:], pos1)
-        nc.sync.dma_start(g1[:], gate[0])
-        nc.sync.dma_start(pos2_sb[:], pos2)
-        nc.sync.dma_start(g2[:], gate[1])
-        load_words(wv_w, wv_words)
-        load_scales(wv_s, wv_scales)
-        for e in range(2, E):
-            load_wk(e)
-
-        for a, b in zip(WORD_CUTS[:-1], WORD_CUTS[1:]):
-            nc.vector.tensor_copy(xw_g[:, a:b], xw[:].bitcast(U32).indirect(offs_sb[:, a // 16 : b // 16]))
-        for a, b in zip(BYTE_CUTS[:-1], BYTE_CUTS[1:]):
-            nc.vector.tensor_copy(xs_g[:, a:b], xs[:].indirect(offs_sb[:, a // 16 : b // 16]))
-
-        def quantise_wk(e):
-            src = wk_raw[e][:].rearrange("p j n -> p n j")
-            if e in VEC_CASTS:
-                nc.vector.tensor_copy(wk_bf[e][:], src)
+        for nm in DMA:
+            if nm == "offs":
+                nc.sync.dma_start(offs_sb[:], offs)
+            elif nm == "xw":
+                nc.sync.dma_start(xw[:], x_words[0].rearrange("p t d -> p (t d)").bitcast(I32))
+            elif nm == "xs":
+                for q in range(4):
+                    nc.sync.dma_start(xs[32 * q : 32 * q + 4, :].bitcast(I32), x_scales[0, 4 * q : 4 * q + 4, :].bitcast(I32))
+            elif nm == "wq":
+                load_words(wq_w, wq_words)
+            elif nm == "wv":
+                load_words(wv_w, wv_words)
+            elif nm == "wqs":
+                load_scales(wq_s, wq_scales)
+            elif nm == "wvs":
+                load_scales(wv_s, wv_scales)
+            elif nm == "bias":
+                nc.sync.dma_start(bias_sb[:, :, 0:E], bias.rearrange("(b p) e -> p b e", p=P))
+            elif nm == "pos1":
+                nc.sync.dma_start(pos1_sb[:], pos1)
+            elif nm == "pos2":
+                nc.sync.dma_start(pos2_sb[:], pos2)
+            elif nm == "g":
+                nc.sync.dma_start(g12[:], gate.rearrange("r p t -> p r t"))
             else:
+                e = int(nm[2])
+                nc.sync.dma_start(wk_raw[e][:], wk[e].rearrange("(p j) n -> p j n", j=4))
+
+        for kind, a, b in XG:
+            if kind == "w":
+                nc.vector.tensor_copy(xw_g[:, a:b], xw[:].bitcast(U32).indirect(offs_sb[:, a // 16 : b // 16]))
+            else:
+                nc.vector.tensor_copy(xs_g[:, a:b], xs[:].indirect(offs_sb[:, a // 16 : b // 16]))
+
+        used = []
+        done = set()
+        y, pa, pb, res, summed = {}, {}, {}, {}, {}
+
+        def bank(width):
+            used.append(width)
+            return psum.tile([P, width], F32, name="acc%d" % len(used), tag="bank%d" % (len(used) % BANKS))
+
+        def fresh(key, width):
+            tag = "own_" + "_".join(str(v) for v in key)
+            for e, tgt in AFTER_C.items():
+                if tgt == key and ("c", e) in done:
+                    tag = "raw%d" % e
+            if key in AFTER_Q and ("q", AFTER_Q[key]) in done:
+                tag = "bf%d" % AFTER_Q[key]
+            return work.tile([P, width], F32, name="t_" + "_".join(str(v) for v in key), tag=tag, align_bytes=64)
+
+        def result(b):
+            if b not in res:
+                res[b] = fresh(("T2", b), T)
+            return res[b]
+
+        def gather(w, b, t0, t1):
+            dst, pos, r = (pa, pos1_sb, 0) if w == "A" else (pb, pos2_sb, 1)
+            if b not in dst:
+                dst[b] = fresh((w, b), T)
+            nc.vector.tensor_tensor(dst[b][:, t0:t1], y[b][:].indirect(pos[:, t0 // 16 : t1 // 16]), g12[:, r, t0:t1], MULT)
+
+        def add(b, t0, t1):
+            nc.vector.tensor_tensor(result(b)[:, t0:t1], pa[b][:, t0:t1], pb[b][:, t0:t1], ADD)
+
+        for step in SEQ:
+            kind = step[0]
+            if kind == "c":
+                e = step[1]
+                src = wk_raw[e][:].rearrange("p j n -> p n j")
                 for h in range(2):
                     nc.scalar.copy(wk_bf[e][:, h * P : (h + 1) * P, :], src[:, h * P : (h + 1) * P, :])
-            nc.vector.quantize_mx(
-                out=wk_w[e][:].bitcast(FP8X4), scales=wk_s[e][:], in_=wk_bf[e][:].rearrange("p n j -> p (n j)")
-            )
-
-        def project(b):
-            which, m = divmod(b, 2)
-            for e in range(E):
-                if which == 1:
-                    w = wk_w[e][:, m * P : (m + 1) * P].bitcast(FP8X4)
-                    ws = wk_s[e][:, m * P : (m + 1) * P]
-                else:
-                    w = (wq_w, None, wv_w)[which][:, e, 2 * m * P : 2 * (m + 1) * P].bitcast(FP4X4)
-                    ws = (wq_s, None, wv_s)[which][:, e, m * P : (m + 1) * P]
-                acc = ypsum.tile([P, C], F32, name="acc")
-                nc.tensor.matmul_mx(
-                    out=acc[:],
-                    lhsT=w,
-                    lhsT_scale=ws,
-                    rhs=xw_g[:, e * C : (e + 1) * C].bitcast(FP8X4),
-                    rhs_scale=xs_g[:, e * C : (e + 1) * C],
-                    start=True,
-                    stop=True,
+            elif kind == "q":
+                e = step[1]
+                nc.vector.quantize_mx(
+                    out=wk_w[e][:].bitcast(FP8X4), scales=wk_s[e][:], in_=wk_bf[e][:].rearrange("p n j -> p (n j)")
                 )
-                nc.scalar.activation(y[b][:, e * C : (e + 1) * C], acc[:], IDENT, bias=bias_sb[:, b, e : e + 1])
-
-        def combine_pe(b):
-            pa = ring.tile([P, T], F32, name="pa")
-            pb = ring.tile([P, T], F32, name="pb")
-            res = ring.tile([P, T], F32, name="res")
-            nc.vector.tensor_tensor(pa[:], y[b][:].indirect(pos1_sb[:]), g1[:], MULT)
-            nc.vector.tensor_tensor(pb[:], y[b][:].indirect(pos2_sb[:]), g2[:], MULT)
-            for h in range(2):
-                turned = tpsum.tile([P, HALF], F32, name="turned")
-                for c in range(HALF // P):
-                    t0 = h * HALF + c * P
-                    nc.tensor.matmul(turned[:, c * P : (c + 1) * P], lhsT=pa[:, t0 : t0 + P], rhs=ident[:], start=True, stop=False, is_transpose=True)
-                    nc.tensor.matmul(turned[:, c * P : (c + 1) * P], lhsT=pb[:, t0 : t0 + P], rhs=ident[:], start=False, stop=True, is_transpose=True)
-                summed = ring.tile([P, HALF], F32, name="summed")
-                nc.scalar.copy(summed[:], turned[:])
-                back = tpsum.tile([P, HALF], F32, name="back")
-                for c in range(HALF // P):
-                    nc.tensor.transpose(back[:, c * P : (c + 1) * P], summed[:, c * P : (c + 1) * P], ident[:])
-                nc.scalar.copy(res[:, h * HALF : (h + 1) * HALF], back[:])
-            nc.sync.dma_start(out[b * P : (b + 1) * P, :], res[:])
-
-        def combine_vec(b, cuts):
-            pa = ring.tile([P, T], F32, name="pa")
-            pb = ring.tile([P, T], F32, name="pb")
-            res = ring.tile([P, T], F32, name="res")
-            for t0, t1 in zip(cuts[:-1], cuts[1:]):
-                nc.vector.tensor_tensor(pa[:, t0:t1], y[b][:].indirect(pos1_sb[:, t0 // 16 : t1 // 16]), g1[:, t0:t1], MULT)
-                nc.vector.tensor_tensor(pb[:, t0:t1], y[b][:].indirect(pos2_sb[:, t0 // 16 : t1 // 16]), g2[:, t0:t1], MULT)
-                nc.vector.tensor_tensor(res[:, t0:t1], pa[:, t0:t1], pb[:, t0:t1], ADD)
-                nc.sync.dma_start(out[b * P : (b + 1) * P, t0:t1], res[:, t0:t1])
-
-        order = (0, 1, 4, 5, 2, 3)
-        quant_after = ((0, 1), (2, 3), (4, 5), (), (), ())
-        project(order[0])
-        for i, b in enumerate(order):
-            if i + 1 < 6 and i + 1 != 4:
-                project(order[i + 1])
-            for e in quant_after[i]:
-                quantise_wk(e)
-            if i + 1 == 4:
-                project(order[i + 1])
-            if i < N_PE:
-                combine_pe(b)
-            elif i < 5:
-                combine_vec(b, (0, T))
+            elif kind == "P":
+                b = step[1]
+                which, m = divmod(b, 2)
+                if b not in y:
+                    y[b] = fresh(("P", b), S)
+                for e in range(3 * step[2], 3 * step[2] + 3):
+                    if which == 1:
+                        w = wk_w[e][:, m * P : (m + 1) * P].bitcast(FP8X4)
+                        ws = wk_s[e][:, m * P : (m + 1) * P]
+                    else:
+                        w = (wq_w, None, wv_w)[which][:, e, 2 * m * P : 2 * (m + 1) * P].bitcast(FP4X4)
+                        ws = (wq_s, None, wv_s)[which][:, e, m * P : (m + 1) * P]
+                    acc = bank(C)
+                    nc.tensor.matmul_mx(
+                        out=acc[:],
+                        lhsT=w,
+                        lhsT_scale=ws,
+                        rhs=xw_g[:, e * C : (e + 1) * C].bitcast(FP8X4),
+                        rhs_scale=xs_g[:, e * C : (e + 1) * C],
+                        start=True,
+                        stop=True,
+                    )
+                    nc.scalar.activation(y[b][:, e * C : (e + 1) * C], acc[:], IDENT, bias=bias_sb[:, b, e : e + 1])
+            elif kind in ("A", "B"):
+                gather(kind, step[1], 0, T)
+            elif kind == "T1":
+                b, t0, t1 = step[1:]
+                turned = bank(t1 - t0)
+                for c in range(t0, t1, P):
+                    nc.tensor.matmul(turned[:, c - t0 : c - t0 + P], lhsT=pa[b][:, c : c + P], rhs=ident[:], start=True, stop=False, is_transpose=True)
+                    nc.tensor.matmul(turned[:, c - t0 : c - t0 + P], lhsT=pb[b][:, c : c + P], rhs=ident[:], start=False, stop=True, is_transpose=True)
+                summed[(b, t0)] = fresh(step, t1 - t0)
+                nc.scalar.copy(summed[(b, t0)][:], turned[:])
+            elif kind == "T2":
+                b, t0, t1 = step[1:]
+                back = bank(t1 - t0)
+                for c in range(0, t1 - t0, P):
+                    nc.tensor.transpose(back[:, c : c + P], summed[(b, t0)][:, c : c + P], ident[:])
+                nc.scalar.copy(result(b)[:, t0:t1], back[:])
+            elif kind == "add":
+                add(step[1], step[2], T)
+            elif kind == "st":
+                b = step[1]
+                nc.sync.dma_start(out[b * P : (b + 1) * P, :], res[b][:])
+            elif kind == "tail1":
+                gather("A", 3, 0, TAIL)
             else:
-                combine_vec(b, TAIL_CUTS)
+                gather("B", 3, 0, TAIL)
+                gather("A", 3, TAIL, T)
+                add(3, 0, TAIL)
+                nc.sync.dma_start(out[3 * P : 4 * P, 0:TAIL], res[3][:, 0:TAIL])
+                gather("B", 3, TAIL, T)
+                add(3, TAIL, T)
+                nc.sync.dma_start(out[3 * P : 4 * P, TAIL:T], res[3][:, TAIL:T])
+            done.add(step)

@@ -21,11 +21,11 @@ IDENT = mybir.ActivationFunctionType.Identity
 
 P = 128
 XG = (('w',0,512),('w',512,1024),('w',1024,1536),('s',0,512),('s',512,1024),('s',1024,1280),('s',1280,1536))
-SEQ = [('c', 2), ('P', 0, 0), ('c', 1), ('P', 0, 1), ('c', 3), ('P', 1, 0), ('P', 1, 1), ('P', 5, 0), ('q', 1), ('A', 0), ('c', 0), ('P', 5, 1), ('q', 0), ('c', 4), ('B', 0), ('T1', 0, 0, 512), ('P', 4, 0), ('q', 2), ('c', 5), ('A', 1), ('P', 2, 0), ('B', 1), ('A', 5), ('q', 4), ('q', 5), ('T1', 1, 0, 512), ('P', 4, 1), ('A', 4), ('q', 3), ('B', 4), ('P', 2, 1), ('P', 3, 0), ('B', 5), ('T2', 0, 0, 512), ('T2', 1, 0, 512), ('A', 2), ('T1', 5, 0, 512), ('T1', 4, 0, 512), ('add', 5, 512), ('P', 3, 1), ('T2', 4, 0, 512), ('B', 2), ('T2', 5, 0, 512), ('add', 2, 512), ('add', 0, 512), ('T1', 2, 0, 512), ('st', 5), ('T2', 2, 0, 512), ('add', 1, 512), ('st', 1), ('add', 4, 512), ('tail1',), ('tail2',), ('st', 4), ('st', 2), ('st', 0)]
-DMA = ['xw', 'offs', 'xs', 'wk0', 'wv', 'wk1', 'wqs', 'wk2', 'pos2', 'wq', 'pos1', 'bias', 'wvs', 'g', 'wk3', 'wk5', 'wk4']
-AFTER_Q = {('A',0): 0, ('B',4): 5, ('B',1): 2, ('B',2): 3, ('A',2): 4}
-AFTER_C = {0: ('T2', 0), 5: ('T2', 4), 3: ('P', 4), 1: ('T1', 1, 0, 512), 4: ('T1', 4, 0, 512)}
-BANKS = 8
+SEQ = [('c', 1), ('c', 2), ('c', 3), ('P', 1, 0), ('c', 0), ('P', 1, 1), ('P', 0, 0), ('P', 5, 0), ('q', 0), ('P', 0, 1), ('P', 5, 1), ('q', 1), ('c', 5), ('A', 5, 0, 768), ('c', 4), ('A', 0, 0, 768), ('q', 4), ('q', 2), ('A', 1, 0, 768), ('B', 0, 0, 768), ('T1', 0, 0, 512), ('P', 2, 0), ('P', 4, 0), ('B', 1, 0, 768), ('P', 4, 1), ('q', 3), ('q', 5), ('T1', 1, 0, 512), ('B', 5, 0, 768), ('P', 2, 1), ('A', 4, 0, 768), ('T1', 5, 0, 512), ('T2', 0, 0, 512), ('T2', 1, 0, 512), ('P', 3, 0), ('A', 2, 0, 768), ('B', 4, 0, 768), ('add', 5, 512, 768), ('add', 1, 512, 768), ('T2', 5, 0, 512), ('P', 3, 1), ('st', 5, 0, 768), ('B', 2, 0, 768), ('add', 4, 512, 768), ('T1', 4, 0, 512), ('add', 0, 512, 768), ('st', 0, 0, 768), ('T1', 2, 0, 512), ('T2', 2, 0, 512), ('st', 1, 0, 768), ('T2', 4, 0, 512), ('add', 2, 512, 768), ('st', 2, 0, 768), ('st', 4, 0, 768), ('A', 3, 0, 512), ('B', 3, 0, 512), ('A', 3, 512, 768), ('add', 3, 0, 512), ('st', 3, 0, 512), ('B', 3, 512, 768), ('add', 3, 512, 768), ('st', 3, 512, 768)]
+DMA = ['xw', 'offs', 'xs', 'wk5', 'wk0', 'wk1', 'wqs', 'wq', 'pos2', 'bias', 'pos1', 'g', 'wk3', 'wvs', 'wv', 'wk2', 'wk4']
+AFTER_Q = {('B', 0): 1, ('A', 1): 0, ('A', 4): 5, ('A', 2): 4}
+AFTER_C = {4: ('P', 1), 1: ('P', 2), 0: ('P', 0), 5: ('T1', 4, 0, 512)}
+BANKS = 7
 TAIL = 512
 
 
@@ -144,9 +144,10 @@ def tile_moe_qkv_kernel(
             kind = step[0]
             if kind == "c":
                 e = step[1]
-                src = wk_raw[e][:].rearrange("p j n -> p n j")
+                src = wk_raw[e][:].rearrange("p j (c i) -> p c j i", i=4)
+                dst = wk_bf[e][:].rearrange("p (c i) j -> p c j i", i=4)
                 for h in range(2):
-                    nc.scalar.copy(wk_bf[e][:, h * P : (h + 1) * P, :], src[:, h * P : (h + 1) * P, :])
+                    nc.scalar.copy(dst[:, h * 32 : (h + 1) * 32, :, :], src[:, h * 32 : (h + 1) * 32, :, :])
             elif kind == "q":
                 e = step[1]
                 nc.vector.quantize_mx(
@@ -176,7 +177,7 @@ def tile_moe_qkv_kernel(
                     )
                     nc.scalar.activation(y[b][:, e * C : (e + 1) * C], acc[:], IDENT, bias=bias_sb[:, b, e : e + 1])
             elif kind in ("A", "B"):
-                gather(kind, step[1], 0, T)
+                gather(kind, step[1], step[2], step[3])
             elif kind == "T1":
                 b, t0, t1 = step[1:]
                 turned = bank(t1 - t0)
@@ -192,18 +193,8 @@ def tile_moe_qkv_kernel(
                     nc.tensor.transpose(back[:, c : c + P], summed[(b, t0)][:, c : c + P], ident[:])
                 nc.scalar.copy(result(b)[:, t0:t1], back[:])
             elif kind == "add":
-                add(step[1], step[2], T)
-            elif kind == "st":
-                b = step[1]
-                nc.sync.dma_start(out[b * P : (b + 1) * P, :], res[b][:])
-            elif kind == "tail1":
-                gather("A", 3, 0, TAIL)
+                add(step[1], step[2], step[3])
             else:
-                gather("B", 3, 0, TAIL)
-                gather("A", 3, TAIL, T)
-                add(3, 0, TAIL)
-                nc.sync.dma_start(out[3 * P : 4 * P, 0:TAIL], res[3][:, 0:TAIL])
-                gather("B", 3, TAIL, T)
-                add(3, TAIL, T)
-                nc.sync.dma_start(out[3 * P : 4 * P, TAIL:T], res[3][:, TAIL:T])
+                b, t0, t1 = step[1:]
+                nc.sync.dma_start(out[b * P : (b + 1) * P, t0:t1], res[b][:, t0:t1])
             done.add(step)

@@ -4,8 +4,8 @@ import concourse.mybir as mybir
 from concourse.masks import make_identity
 
 K, T, E, C, N = 512, 768, 6, 256, 256
-S = E * C
-FLOPS = 2 * K * S * 3 * N
+SLOTS = E * C
+FLOPS = 2 * K * SLOTS * 3 * N
 
 F32 = mybir.dt.float32
 BF16 = mybir.dt.bfloat16
@@ -17,16 +17,19 @@ FP8X4 = mybir.dt.float8_e4m3fn_x4
 FP4X4 = mybir.dt.float4_e2m1fn_x4
 MULT = mybir.AluOpType.mult
 ADD = mybir.AluOpType.add
-IDENT = mybir.ActivationFunctionType.Identity
+IDENTITY = mybir.ActivationFunctionType.Identity
 
 P = 128
-XG = (('w',0,512),('w',512,1024),('w',1024,1536),('s',0,512),('s',512,1024),('s',1024,1280),('s',1280,1536))
-SEQ = [('c', 1), ('c', 2), ('c', 3), ('P', 1, 0), ('c', 0), ('P', 1, 1), ('P', 0, 0), ('P', 5, 0), ('q', 0), ('P', 0, 1), ('P', 5, 1), ('q', 1), ('c', 5), ('A', 5, 0, 768), ('c', 4), ('A', 0, 0, 768), ('q', 4), ('q', 2), ('A', 1, 0, 768), ('B', 0, 0, 768), ('T1', 0, 0, 512), ('P', 2, 0), ('P', 4, 0), ('B', 1, 0, 768), ('P', 4, 1), ('q', 3), ('q', 5), ('T1', 1, 0, 512), ('B', 5, 0, 768), ('P', 2, 1), ('A', 4, 0, 768), ('T1', 5, 0, 512), ('T2', 0, 0, 512), ('T2', 1, 0, 512), ('P', 3, 0), ('A', 2, 0, 768), ('B', 4, 0, 768), ('add', 5, 512, 768), ('add', 1, 512, 768), ('T2', 5, 0, 512), ('P', 3, 1), ('st', 5, 0, 768), ('B', 2, 0, 768), ('add', 4, 512, 768), ('T1', 4, 0, 512), ('add', 0, 512, 768), ('st', 0, 0, 768), ('T1', 2, 0, 512), ('T2', 2, 0, 512), ('st', 1, 0, 768), ('T2', 4, 0, 512), ('add', 2, 512, 768), ('st', 2, 0, 768), ('st', 4, 0, 768), ('A', 3, 0, 512), ('B', 3, 0, 512), ('A', 3, 512, 768), ('add', 3, 0, 512), ('st', 3, 0, 512), ('B', 3, 512, 768), ('add', 3, 512, 768), ('st', 3, 512, 768)]
-DMA = ['xw', 'offs', 'xs', 'wk5', 'wk0', 'wk1', 'wqs', 'wq', 'pos2', 'bias', 'pos1', 'g', 'wk3', 'wvs', 'wv', 'wk2', 'wk4']
-AFTER_Q = {('B', 0): 1, ('A', 1): 0, ('A', 4): 5, ('A', 2): 4}
-AFTER_C = {4: ('P', 1), 1: ('P', 2), 0: ('P', 0), 5: ('T1', 4, 0, 512)}
-BANKS = 7
-TAIL = 512
+PACK = 4
+PER_COLUMN = 16
+BLOCKS = 3 * N // P
+Q0, Q1, K0, K1, V0, V1 = range(BLOCKS)
+BANKS = 8
+BIAS_PITCH = 8
+BYTE_CUTS = (0, 512, 1024, SLOTS)
+WORD_CUTS = (0, 512, 1024, 1280, SLOTS)
+HALVES = (slice(0, T // 2), slice(T // 2, T))
+HEAD, TAIL, ALL = slice(0, 512), slice(512, T), slice(0, T)
 
 
 def tile_moe_qkv_kernel(
@@ -35,166 +38,192 @@ def tile_moe_qkv_kernel(
     nc = tc.nc
     with ExitStack() as ctx:
         keep = ctx.enter_context(tc.tile_pool(name="keep", bufs=1))
-        work = ctx.enter_context(tc.tile_pool(name="work", bufs=1))
         psum = ctx.enter_context(tc.psum_pool(name="psum", bufs=1))
 
-        offs_sb = keep.tile([P, S // 16], U16, name="offs_sb")
-        pos1_sb = keep.tile([P, T // 16], U16, name="pos1_sb")
-        pos2_sb = keep.tile([P, T // 16], U16, name="pos2_sb")
-        xw = keep.tile([P, T], I32, name="xw", align_bytes=64)
-        xs = keep.tile([P, T], U8, name="xs", align_bytes=64)
-        xw_g = keep.tile([P, S], U32, name="xw_g", align_bytes=64)
-        xs_g = keep.tile([P, S], U8, name="xs_g", align_bytes=64)
-        wq_w = keep.tile([P, E, 2 * N], U8, name="wq_w", align_bytes=64)
-        wv_w = keep.tile([P, E, 2 * N], U8, name="wv_w", align_bytes=64)
-        wq_s = keep.tile([P, E, N], U8, name="wq_s", align_bytes=64)
-        wv_s = keep.tile([P, E, N], U8, name="wv_s", align_bytes=64)
-        wk_raw = [work.tile([P, 4, N], F32, name="wk_raw%d" % e, tag="raw%d" % e, align_bytes=64) for e in range(E)]
-        wk_bf = [work.tile([P, N, 4], BF16, name="wk_bf%d" % e, tag="bf%d" % e, align_bytes=64) for e in range(E)]
-        wk_w = [keep.tile([P, N], U32, name="wk_w%d" % e, align_bytes=64) for e in range(E)]
-        wk_s = [keep.tile([P, N], U8, name="wk_s%d" % e, align_bytes=64) for e in range(E)]
-        bias_sb = keep.tile([P, 6, 8], F32, name="bias_sb")
-        g12 = keep.tile([P, 2, T], F32, name="g12")
+        def tiles(name, count, shape, dtype):
+            return [keep.tile(shape, dtype, name="%s%d" % (name, i), align_bytes=64) for i in range(count)]
+
+        offs_sb = keep.tile([P, SLOTS // PER_COLUMN], U16, name="offs_sb")
+        pos_sb = tiles("pos_sb", 2, [P, T // PER_COLUMN], U16)
+        gate_sb = tiles("gate_sb", 2, [P, T], F32)
+        bias_sb = keep.tile([P, BLOCKS, BIAS_PITCH], F32, name="bias_sb")
+        token_words = keep.tile([P, T], I32, name="token_words", align_bytes=64)
+        token_scales = keep.tile([P, T], U8, name="token_scales", align_bytes=64)
+        slot_words = keep.tile([P, SLOTS], U32, name="slot_words", align_bytes=64)
+        slot_scales = keep.tile([P, SLOTS], U8, name="slot_scales", align_bytes=64)
+        wq_w, wv_w = tiles("fp4_words", 2, [P, E, 2 * N], U8)
+        wq_s, wv_s = tiles("fp4_scales", 2, [P, E, N], U8)
+        wk_raw = tiles("wk_raw", E, [P, PACK, N], F32)
+        wk_bf = tiles("wk_bf", E, [P, N, PACK], BF16)
+        wk_w = tiles("wk_w", E, [P, N], U32)
+        wk_s = tiles("wk_s", E, [P, N], U8)
+        y = tiles("y", BLOCKS, [P, SLOTS], F32)
+        gated = [tiles("gated%d_" % r, BLOCKS, [P, T], F32) for r in range(2)]
+        result = tiles("result", BLOCKS, [P, T], F32)
+        turned_sum = {b: tiles("turned_sum%d_" % b, 2, [P, T // 2], F32) for b in (Q0, Q1, V0, V1)}
         ident = keep.tile([P, P], F32, name="ident")
         warm = keep.tile([P, 8], F32, name="warm")
 
-        nc.vector.memset(xs[:].bitcast(I32), 0)
+        nc.gpsimd.memset(token_scales[:].bitcast(I32), 0)
         nc.vector.memset(warm[:, 0:1], 0.0)
-        nc.scalar.activation(warm[:, 4:5], warm[:, 0:1], IDENT)
-        nc.vector.memset(wq_s[:].rearrange("p e n -> p (e n)").bitcast(I32), 0)
-        nc.vector.memset(wv_s[:].rearrange("p e n -> p (e n)").bitcast(I32), 0)
+        nc.scalar.activation(warm[:, 4:5], warm[:, 0:1], IDENTITY)
+        for scales in (wq_s, wv_s):
+            nc.vector.memset(scales[:].rearrange("p e n -> p (e n)").bitcast(I32), 0)
         make_identity(nc, ident[:])
 
-        def load_words(dst, src):
+        def load_fp4_words(dst, src):
             nc.sync.dma_start(dst[:].bitcast(I32), src.rearrange("e s p b -> p (e s) b").bitcast(I32))
 
-        def load_scales(dst, src):
+        def load_fp4_scales(dst, src):
             for q in range(4):
-                nc.sync.dma_start(
-                    dst[32 * q : 32 * q + 4, :, :].bitcast(I32),
-                    src[:, 0, 4 * q : 4 * q + 4, :].rearrange("e i n -> i e n").bitcast(I32),
-                )
+                rows = src[:, 0, 4 * q : 4 * q + 4, :].rearrange("e i n -> i e n")
+                nc.sync.dma_start(dst[32 * q : 32 * q + 4, :, :].bitcast(I32), rows.bitcast(I32))
 
-        for nm in DMA:
-            if nm == "offs":
-                nc.sync.dma_start(offs_sb[:], offs)
-            elif nm == "xw":
-                nc.sync.dma_start(xw[:], x_words[0].rearrange("p t d -> p (t d)").bitcast(I32))
-            elif nm == "xs":
-                for q in range(4):
-                    nc.sync.dma_start(xs[32 * q : 32 * q + 4, :].bitcast(I32), x_scales[0, 4 * q : 4 * q + 4, :].bitcast(I32))
-            elif nm == "wq":
-                load_words(wq_w, wq_words)
-            elif nm == "wv":
-                load_words(wv_w, wv_words)
-            elif nm == "wqs":
-                load_scales(wq_s, wq_scales)
-            elif nm == "wvs":
-                load_scales(wv_s, wv_scales)
-            elif nm == "bias":
-                nc.sync.dma_start(bias_sb[:, :, 0:E], bias.rearrange("(b p) e -> p b e", p=P))
-            elif nm == "pos1":
-                nc.sync.dma_start(pos1_sb[:], pos1)
-            elif nm == "pos2":
-                nc.sync.dma_start(pos2_sb[:], pos2)
-            elif nm == "g":
-                nc.sync.dma_start(g12[:], gate.rearrange("r p t -> p r t"))
-            else:
-                e = int(nm[2])
-                nc.sync.dma_start(wk_raw[e][:], wk[e].rearrange("(p j) n -> p j n", j=4))
+        def load_wk(e):
+            nc.sync.dma_start(wk_raw[e][:], wk[e].rearrange("(p j) n -> p j n", j=PACK))
 
-        for kind, a, b in XG:
-            if kind == "w":
-                nc.vector.tensor_copy(xw_g[:, a:b], xw[:].bitcast(U32).indirect(offs_sb[:, a // 16 : b // 16]))
-            else:
-                nc.vector.tensor_copy(xs_g[:, a:b], xs[:].indirect(offs_sb[:, a // 16 : b // 16]))
+        nc.sync.dma_start(offs_sb[:], offs)
+        for q in range(4):
+            nc.sync.dma_start(
+                token_scales[32 * q : 32 * q + 4, :].bitcast(I32), x_scales[0, 4 * q : 4 * q + 4, :].bitcast(I32)
+            )
+        nc.sync.dma_start(token_words[:], x_words[0].rearrange("p t d -> p (t d)").bitcast(I32))
+        load_wk(0)
+        load_wk(1)
+        load_fp4_scales(wq_s, wq_scales)
+        load_fp4_words(wq_w, wq_words)
+        nc.sync.dma_start(bias_sb[:, :, 0:E], bias.rearrange("(b p) e -> p b e", p=P))
+        for r, pos in enumerate((pos1, pos2)):
+            nc.sync.dma_start(pos_sb[r][:], pos)
+            nc.sync.dma_start(gate_sb[r][:], gate[r])
+        load_wk(2)
+        load_fp4_scales(wv_s, wv_scales)
+        load_fp4_words(wv_w, wv_words)
+        for e in range(3, E):
+            load_wk(e)
 
-        used = []
-        done = set()
-        y, pa, pb, res, summed = {}, {}, {}, {}, {}
+        def entries(list_sb, a, b):
+            return list_sb[:, a // PER_COLUMN : b // PER_COLUMN]
+
+        for a, b in zip(BYTE_CUTS[:-1], BYTE_CUTS[1:]):
+            nc.vector.tensor_copy(slot_scales[:, a:b], token_scales[:].indirect(entries(offs_sb, a, b)))
+        for a, b in zip(WORD_CUTS[:-1], WORD_CUTS[1:]):
+            nc.vector.tensor_copy(slot_words[:, a:b], token_words[:].bitcast(U32).indirect(entries(offs_sb, a, b)))
+
+        taken = []
 
         def bank(width):
-            used.append(width)
-            return psum.tile([P, width], F32, name="acc%d" % len(used), tag="bank%d" % (len(used) % BANKS))
+            taken.append(width)
+            return psum.tile([P, width], F32, name="acc%d" % len(taken), tag="bank%d" % (len(taken) % BANKS))
 
-        def fresh(key, width):
-            tag = "own_" + "_".join(str(v) for v in key)
-            for e, tgt in AFTER_C.items():
-                if tgt == key and ("c", e) in done:
-                    tag = "raw%d" % e
-            if key in AFTER_Q and ("q", AFTER_Q[key]) in done:
-                tag = "bf%d" % AFTER_Q[key]
-            return work.tile([P, width], F32, name="t_" + "_".join(str(v) for v in key), tag=tag, align_bytes=64)
+        def quantise_wk(e):
+            src = wk_raw[e][:].rearrange("p j (c i) -> p c j i", i=4)
+            dst = wk_bf[e][:].rearrange("p (c i) j -> p c j i", i=4)
+            for groups in (slice(0, N // 8), slice(N // 8, N // 4)):
+                nc.scalar.copy(dst[:, groups, :, :], src[:, groups, :, :])
+            nc.vector.quantize_mx(
+                out=wk_w[e][:].bitcast(FP8X4), scales=wk_s[e][:], in_=wk_bf[e][:].rearrange("p n j -> p (n j)")
+            )
 
-        def result(b):
-            if b not in res:
-                res[b] = fresh(("T2", b), T)
-            return res[b]
-
-        def gather(w, b, t0, t1):
-            dst, pos, r = (pa, pos1_sb, 0) if w == "A" else (pb, pos2_sb, 1)
-            if b not in dst:
-                dst[b] = fresh((w, b), T)
-            nc.vector.tensor_tensor(dst[b][:, t0:t1], y[b][:].indirect(pos[:, t0 // 16 : t1 // 16]), g12[:, r, t0:t1], MULT)
-
-        def add(b, t0, t1):
-            nc.vector.tensor_tensor(result(b)[:, t0:t1], pa[b][:, t0:t1], pb[b][:, t0:t1], ADD)
-
-        for step in SEQ:
-            kind = step[0]
-            if kind == "c":
-                e = step[1]
-                src = wk_raw[e][:].rearrange("p j (c i) -> p c j i", i=4)
-                dst = wk_bf[e][:].rearrange("p (c i) j -> p c j i", i=4)
-                for h in range(2):
-                    nc.scalar.copy(dst[:, h * 32 : (h + 1) * 32, :, :], src[:, h * 32 : (h + 1) * 32, :, :])
-            elif kind == "q":
-                e = step[1]
-                nc.vector.quantize_mx(
-                    out=wk_w[e][:].bitcast(FP8X4), scales=wk_s[e][:], in_=wk_bf[e][:].rearrange("p n j -> p (n j)")
+        def project(b, experts=range(E)):
+            cols = slice(b % 2 * P, (b % 2 + 1) * P)
+            for e in experts:
+                if b in (K0, K1):
+                    w, w_scale = wk_w[e][:, cols].bitcast(FP8X4), wk_s[e][:, cols]
+                else:
+                    words, scales = (wq_w, wq_s) if b in (Q0, Q1) else (wv_w, wv_s)
+                    w, w_scale = words[:, e, 2 * cols.start : 2 * cols.stop].bitcast(FP4X4), scales[:, e, cols]
+                slots = slice(e * C, (e + 1) * C)
+                acc = bank(C)
+                nc.tensor.matmul_mx(
+                    out=acc[:],
+                    lhsT=w,
+                    lhsT_scale=w_scale,
+                    rhs=slot_words[:, slots].bitcast(FP8X4),
+                    rhs_scale=slot_scales[:, slots],
+                    start=True,
+                    stop=True,
                 )
-            elif kind == "P":
-                b = step[1]
-                which, m = divmod(b, 2)
-                if b not in y:
-                    y[b] = fresh(("P", b), S)
-                for e in range(3 * step[2], 3 * step[2] + 3):
-                    if which == 1:
-                        w = wk_w[e][:, m * P : (m + 1) * P].bitcast(FP8X4)
-                        ws = wk_s[e][:, m * P : (m + 1) * P]
-                    else:
-                        w = (wq_w, None, wv_w)[which][:, e, 2 * m * P : 2 * (m + 1) * P].bitcast(FP4X4)
-                        ws = (wq_s, None, wv_s)[which][:, e, m * P : (m + 1) * P]
-                    acc = bank(C)
-                    nc.tensor.matmul_mx(
-                        out=acc[:],
-                        lhsT=w,
-                        lhsT_scale=ws,
-                        rhs=xw_g[:, e * C : (e + 1) * C].bitcast(FP8X4),
-                        rhs_scale=xs_g[:, e * C : (e + 1) * C],
-                        start=True,
-                        stop=True,
-                    )
-                    nc.scalar.activation(y[b][:, e * C : (e + 1) * C], acc[:], IDENT, bias=bias_sb[:, b, e : e + 1])
-            elif kind in ("A", "B"):
-                gather(kind, step[1], step[2], step[3])
-            elif kind == "T1":
-                b, t0, t1 = step[1:]
-                turned = bank(t1 - t0)
-                for c in range(t0, t1, P):
-                    nc.tensor.matmul(turned[:, c - t0 : c - t0 + P], lhsT=pa[b][:, c : c + P], rhs=ident[:], start=True, stop=False, is_transpose=True)
-                    nc.tensor.matmul(turned[:, c - t0 : c - t0 + P], lhsT=pb[b][:, c : c + P], rhs=ident[:], start=False, stop=True, is_transpose=True)
-                summed[(b, t0)] = fresh(step, t1 - t0)
-                nc.scalar.copy(summed[(b, t0)][:], turned[:])
-            elif kind == "T2":
-                b, t0, t1 = step[1:]
-                back = bank(t1 - t0)
-                for c in range(0, t1 - t0, P):
-                    nc.tensor.transpose(back[:, c : c + P], summed[(b, t0)][:, c : c + P], ident[:])
-                nc.scalar.copy(result(b)[:, t0:t1], back[:])
-            elif kind == "add":
-                add(step[1], step[2], step[3])
-            else:
-                b, t0, t1 = step[1:]
-                nc.sync.dma_start(out[b * P : (b + 1) * P, t0:t1], res[b][:, t0:t1])
-            done.add(step)
+                nc.scalar.activation(y[b][:, slots], acc[:], IDENTITY, bias=bias_sb[:, b, e : e + 1])
+
+        def gather(r, b, tokens):
+            picked = y[b][:].indirect(entries(pos_sb[r], tokens.start, tokens.stop))
+            nc.vector.tensor_tensor(gated[r][b][:, tokens], picked, gate_sb[r][:, tokens], MULT)
+
+        def gather_both(b):
+            gather(0, b, ALL)
+            gather(1, b, ALL)
+
+        def add_turned(b):
+            for h, tokens in enumerate(HALVES):
+                acc = bank(T // 2)
+                for t in range(0, T // 2, P):
+                    for r in range(2):
+                        nc.tensor.matmul(
+                            acc[:, t : t + P],
+                            lhsT=gated[r][b][:, tokens.start + t : tokens.start + t + P],
+                            rhs=ident[:],
+                            start=(r == 0),
+                            stop=(r == 1),
+                            is_transpose=True,
+                        )
+                nc.scalar.copy(turned_sum[b][h][:], acc[:])
+
+        def turn_back(b, h):
+            acc = bank(T // 2)
+            for t in range(0, T // 2, P):
+                nc.tensor.transpose(acc[:, t : t + P], turned_sum[b][h][:, t : t + P], ident[:])
+            nc.scalar.copy(result[b][:, HALVES[h]], acc[:])
+
+        def add(b, tokens):
+            nc.vector.tensor_tensor(result[b][:, tokens], gated[0][b][:, tokens], gated[1][b][:, tokens], ADD)
+
+        def store(queue, b, tokens):
+            queue.dma_start(out[b * P : (b + 1) * P, tokens], result[b][:, tokens])
+
+        quantise_wk(0)
+        quantise_wk(1)
+        project(Q0)
+        project(Q1)
+        quantise_wk(2)
+        project(V0)
+        project(V1, range(0, E // 2))
+        for e in range(3, E):
+            quantise_wk(e)
+        project(V1, range(E // 2, E))
+
+        gather_both(Q0)
+        gather_both(Q1)
+        add_turned(Q0)
+        add_turned(Q1)
+        gather_both(V0)
+        project(K0)
+        for b in (Q0, Q1):
+            turn_back(b, 0)
+            turn_back(b, 1)
+            store(nc.sync, b, ALL)
+        gather_both(V1)
+        add_turned(V0)
+        project(K1)
+        turn_back(V0, 0)
+        turn_back(V0, 1)
+        store(nc.scalar, V0, ALL)
+        add_turned(V1)
+        for h, tokens in enumerate(HALVES):
+            turn_back(V1, h)
+            store(nc.scalar, V1, tokens)
+
+        gather(0, K0, ALL)
+        gather(1, K0, HEAD)
+        gather(1, K0, TAIL)
+        add(K0, HEAD)
+        add(K0, TAIL)
+        store(nc.sync, K0, ALL)
+        gather(0, K1, HEAD)
+        gather(1, K1, HEAD)
+        gather(0, K1, TAIL)
+        add(K1, HEAD)
+        store(nc.sync, K1, HEAD)
+        gather(1, K1, TAIL)
+        add(K1, TAIL)
+        store(nc.sync, K1, TAIL)

@@ -24,10 +24,13 @@ PACK = 4
 PER_COLUMN = 16
 BLOCKS = 3 * N // P
 Q0, Q1, K0, K1, V0, V1 = range(BLOCKS)
+LAST_GATHERS = (0, 512, 768)
+LAST_ADDS = (0, 256, 512, 768)
 BANKS = 8
 BIAS_PITCH = 8
-BYTE_CUTS = (0, 512, 1024, SLOTS)
-WORD_CUTS = (0, 512, 1024, 1280, SLOTS)
+BYTE_WINDOW = 2048
+WORD_WINDOW = 1024
+WORD_CUTS = (0, 768, 1152, 1408, SLOTS)
 HALVES = (slice(0, T // 2), slice(T // 2, T))
 HEAD, TAIL, ALL = slice(0, 512), slice(512, T), slice(0, T)
 
@@ -47,8 +50,8 @@ def tile_moe_qkv_kernel(
         pos_sb = tiles("pos_sb", 2, [P, T // PER_COLUMN], U16)
         gate_sb = tiles("gate_sb", 2, [P, T], F32)
         bias_sb = keep.tile([P, BLOCKS, BIAS_PITCH], F32, name="bias_sb")
-        token_words = keep.tile([P, T], I32, name="token_words", align_bytes=64)
-        token_scales = keep.tile([P, T], U8, name="token_scales", align_bytes=64)
+        token_words = keep.tile([P, WORD_WINDOW], I32, name="token_words", align_bytes=64)
+        token_scales = keep.tile([P, BYTE_WINDOW], U8, name="token_scales", align_bytes=64)
         slot_words = keep.tile([P, SLOTS], U32, name="slot_words", align_bytes=64)
         slot_scales = keep.tile([P, SLOTS], U8, name="slot_scales", align_bytes=64)
         wq_w, wv_w = tiles("fp4_words", 2, [P, E, 2 * N], U8)
@@ -64,9 +67,11 @@ def tile_moe_qkv_kernel(
         ident = keep.tile([P, P], F32, name="ident")
         warm = keep.tile([P, 8], F32, name="warm")
 
-        nc.gpsimd.memset(token_scales[:].bitcast(I32), 0)
+        nc.gpsimd.memset(token_scales[:, 0:T].bitcast(I32), 0)
         nc.vector.memset(warm[:, 0:1], 0.0)
         nc.scalar.activation(warm[:, 4:5], warm[:, 0:1], IDENTITY)
+        nc.vector.memset(token_scales[:, T:BYTE_WINDOW].bitcast(I32), 0)
+        nc.vector.memset(token_words[:, T:WORD_WINDOW], 0)
         for scales in (wq_s, wv_s):
             nc.vector.memset(scales[:].rearrange("p e n -> p (e n)").bitcast(I32), 0)
         make_identity(nc, ident[:])
@@ -75,19 +80,17 @@ def tile_moe_qkv_kernel(
             nc.sync.dma_start(dst[:].bitcast(I32), src.rearrange("e s p b -> p (e s) b").bitcast(I32))
 
         def load_fp4_scales(dst, src):
-            for q in range(4):
-                rows = src[:, 0, 4 * q : 4 * q + 4, :].rearrange("e i n -> i e n")
-                nc.sync.dma_start(dst[32 * q : 32 * q + 4, :, :].bitcast(I32), rows.bitcast(I32))
+            for i in range(4):
+                rows = src[:, 0, i::4, :].rearrange("e q n -> q e n")
+                nc.sync.dma_start(dst[i:P:32, :, :].bitcast(I32), rows.bitcast(I32))
 
         def load_wk(e):
             nc.sync.dma_start(wk_raw[e][:], wk[e].rearrange("(p j) n -> p j n", j=PACK))
 
         nc.sync.dma_start(offs_sb[:], offs)
-        for q in range(4):
-            nc.sync.dma_start(
-                token_scales[32 * q : 32 * q + 4, :].bitcast(I32), x_scales[0, 4 * q : 4 * q + 4, :].bitcast(I32)
-            )
-        nc.sync.dma_start(token_words[:], x_words[0].rearrange("p t d -> p (t d)").bitcast(I32))
+        for i in range(4):
+            nc.sync.dma_start(token_scales[i:P:32, 0:T].bitcast(I32), x_scales[0, i::4, :].bitcast(I32))
+        nc.sync.dma_start(token_words[:, 0:T], x_words[0].rearrange("p t d -> p (t d)").bitcast(I32))
         load_wk(0)
         load_wk(1)
         load_fp4_scales(wq_s, wq_scales)
@@ -105,8 +108,7 @@ def tile_moe_qkv_kernel(
         def entries(list_sb, a, b):
             return list_sb[:, a // PER_COLUMN : b // PER_COLUMN]
 
-        for a, b in zip(BYTE_CUTS[:-1], BYTE_CUTS[1:]):
-            nc.vector.tensor_copy(slot_scales[:, a:b], token_scales[:].indirect(entries(offs_sb, a, b)))
+        nc.vector.tensor_copy(slot_scales[:], token_scales[:].indirect(offs_sb[:]))
         for a, b in zip(WORD_CUTS[:-1], WORD_CUTS[1:]):
             nc.vector.tensor_copy(slot_words[:, a:b], token_words[:].bitcast(U32).indirect(entries(offs_sb, a, b)))
 
@@ -125,16 +127,21 @@ def tile_moe_qkv_kernel(
                 out=wk_w[e][:].bitcast(FP8X4), scales=wk_s[e][:], in_=wk_bf[e][:].rearrange("p n j -> p (n j)")
             )
 
-        def project(b, experts=range(E)):
+        def pieces(experts, cuts):
+            borders = sorted(set(range(experts.start * C, experts.stop * C + 1, C)) | set(cuts))
+            return zip(borders[:-1], borders[1:])
+
+        def project(b, experts=range(E), cuts=()):
             cols = slice(b % 2 * P, (b % 2 + 1) * P)
-            for e in experts:
+            for first, last in pieces(experts, cuts):
+                e = first // C
                 if b in (K0, K1):
                     w, w_scale = wk_w[e][:, cols].bitcast(FP8X4), wk_s[e][:, cols]
                 else:
                     words, scales = (wq_w, wq_s) if b in (Q0, Q1) else (wv_w, wv_s)
                     w, w_scale = words[:, e, 2 * cols.start : 2 * cols.stop].bitcast(FP4X4), scales[:, e, cols]
-                slots = slice(e * C, (e + 1) * C)
-                acc = bank(C)
+                slots = slice(first, last)
+                acc = bank(last - first)
                 nc.tensor.matmul_mx(
                     out=acc[:],
                     lhsT=w,
@@ -183,7 +190,7 @@ def tile_moe_qkv_kernel(
 
         quantise_wk(0)
         quantise_wk(1)
-        project(Q0)
+        project(Q0, cuts=WORD_CUTS)
         project(Q1)
         quantise_wk(2)
         project(V0)
@@ -219,11 +226,9 @@ def tile_moe_qkv_kernel(
         add(K0, HEAD)
         add(K0, TAIL)
         store(nc.sync, K0, ALL)
-        gather(0, K1, HEAD)
-        gather(1, K1, HEAD)
-        gather(0, K1, TAIL)
-        add(K1, HEAD)
-        store(nc.sync, K1, HEAD)
-        gather(1, K1, TAIL)
-        add(K1, TAIL)
-        store(nc.sync, K1, TAIL)
+        gather(0, K1, ALL)
+        for a, b in zip(LAST_GATHERS[:-1], LAST_GATHERS[1:]):
+            gather(1, K1, slice(a, b))
+        for a, b in zip(LAST_ADDS[:-1], LAST_ADDS[1:]):
+            add(K1, slice(a, b))
+            store(nc.sync, K1, slice(a, b))

@@ -24,15 +24,14 @@ PACK = 4
 PER_COLUMN = 16
 BLOCKS = 3 * N // P
 Q0, Q1, K0, K1, V0, V1 = range(BLOCKS)
-LAST_GATHERS = (0, 512, 768)
-LAST_ADDS = (0, 256, 512, 768)
 BANKS = 8
 BIAS_PITCH = 8
+QUADRANT = 32
 BYTE_WINDOW = 2048
-WORD_WINDOW = 1024
-WORD_CUTS = (0, 768, 1152, 1408, SLOTS)
+WORD_CUTS = (0, 512, 1024, 1280, 1408, SLOTS)
 HALVES = (slice(0, T // 2), slice(T // 2, T))
 HEAD, TAIL, ALL = slice(0, 512), slice(512, T), slice(0, T)
+THIRDS = tuple(slice(t, t + T // 3) for t in range(0, T, T // 3))
 
 
 def tile_moe_qkv_kernel(
@@ -50,7 +49,7 @@ def tile_moe_qkv_kernel(
         pos_sb = tiles("pos_sb", 2, [P, T // PER_COLUMN], U16)
         gate_sb = tiles("gate_sb", 2, [P, T], F32)
         bias_sb = keep.tile([P, BLOCKS, BIAS_PITCH], F32, name="bias_sb")
-        token_words = keep.tile([P, WORD_WINDOW], I32, name="token_words", align_bytes=64)
+        token_words = keep.tile([P, T], I32, name="token_words", align_bytes=64)
         token_scales = keep.tile([P, BYTE_WINDOW], U8, name="token_scales", align_bytes=64)
         slot_words = keep.tile([P, SLOTS], U32, name="slot_words", align_bytes=64)
         slot_scales = keep.tile([P, SLOTS], U8, name="slot_scales", align_bytes=64)
@@ -71,7 +70,6 @@ def tile_moe_qkv_kernel(
         nc.vector.memset(warm[:, 0:1], 0.0)
         nc.scalar.activation(warm[:, 4:5], warm[:, 0:1], IDENTITY)
         nc.vector.memset(token_scales[:, T:BYTE_WINDOW].bitcast(I32), 0)
-        nc.vector.memset(token_words[:, T:WORD_WINDOW], 0)
         for scales in (wq_s, wv_s):
             nc.vector.memset(scales[:].rearrange("p e n -> p (e n)").bitcast(I32), 0)
         make_identity(nc, ident[:])
@@ -82,15 +80,15 @@ def tile_moe_qkv_kernel(
         def load_fp4_scales(dst, src):
             for i in range(4):
                 rows = src[:, 0, i::4, :].rearrange("e q n -> q e n")
-                nc.sync.dma_start(dst[i:P:32, :, :].bitcast(I32), rows.bitcast(I32))
+                nc.sync.dma_start(dst[i:P:QUADRANT, :, :].bitcast(I32), rows.bitcast(I32))
 
         def load_wk(e):
             nc.sync.dma_start(wk_raw[e][:], wk[e].rearrange("(p j) n -> p j n", j=PACK))
 
         nc.sync.dma_start(offs_sb[:], offs)
         for i in range(4):
-            nc.sync.dma_start(token_scales[i:P:32, 0:T].bitcast(I32), x_scales[0, i::4, :].bitcast(I32))
-        nc.sync.dma_start(token_words[:, 0:T], x_words[0].rearrange("p t d -> p (t d)").bitcast(I32))
+            nc.sync.dma_start(token_scales[i:P:QUADRANT, 0:T].bitcast(I32), x_scales[0, i::4, :].bitcast(I32))
+        nc.sync.dma_start(token_words[:], x_words[0].rearrange("p t d -> p (t d)").bitcast(I32))
         load_wk(0)
         load_wk(1)
         load_fp4_scales(wq_s, wq_scales)
@@ -105,12 +103,13 @@ def tile_moe_qkv_kernel(
         for e in range(3, E):
             load_wk(e)
 
-        def entries(list_sb, a, b):
-            return list_sb[:, a // PER_COLUMN : b // PER_COLUMN]
+        def entries(list_sb, first, last):
+            return list_sb[:, first // PER_COLUMN : last // PER_COLUMN]
 
         nc.vector.tensor_copy(slot_scales[:], token_scales[:].indirect(offs_sb[:]))
-        for a, b in zip(WORD_CUTS[:-1], WORD_CUTS[1:]):
-            nc.vector.tensor_copy(slot_words[:, a:b], token_words[:].bitcast(U32).indirect(entries(offs_sb, a, b)))
+        for first, last in zip(WORD_CUTS[:-1], WORD_CUTS[1:]):
+            picked = token_words[:].bitcast(U32).indirect(entries(offs_sb, first, last))
+            nc.vector.tensor_copy(slot_words[:, first:last], picked)
 
         taken = []
 
@@ -227,8 +226,8 @@ def tile_moe_qkv_kernel(
         add(K0, TAIL)
         store(nc.sync, K0, ALL)
         gather(0, K1, ALL)
-        for a, b in zip(LAST_GATHERS[:-1], LAST_GATHERS[1:]):
-            gather(1, K1, slice(a, b))
-        for a, b in zip(LAST_ADDS[:-1], LAST_ADDS[1:]):
-            add(K1, slice(a, b))
-            store(nc.sync, K1, slice(a, b))
+        gather(1, K1, HEAD)
+        gather(1, K1, TAIL)
+        for tokens in THIRDS:
+            add(K1, tokens)
+            store(nc.sync, K1, tokens)

@@ -24,11 +24,12 @@ PACK = 4
 PER_COLUMN = 16
 BLOCKS = 3 * N // P
 Q0, Q1, K0, K1, V0, V1 = range(BLOCKS)
-BANKS = 8
+RING = 5
 BIAS_PITCH = 8
 QUADRANT = 32
 BYTE_WINDOW = 2048
-WORD_CUTS = (0, 512, 1024, 1280, 1408, SLOTS)
+WORD_CUTS = (0, 512, 1024, 1280, SLOTS)
+WORD_WINDOW = 1024
 HALVES = (slice(0, T // 2), slice(T // 2, T))
 HEAD, TAIL, ALL = slice(0, 512), slice(512, T), slice(0, T)
 THIRDS = tuple(slice(t, t + T // 3) for t in range(0, T, T // 3))
@@ -49,7 +50,7 @@ def tile_moe_qkv_kernel(
         pos_sb = tiles("pos_sb", 2, [P, T // PER_COLUMN], U16)
         gate_sb = tiles("gate_sb", 2, [P, T], F32)
         bias_sb = keep.tile([P, BLOCKS, BIAS_PITCH], F32, name="bias_sb")
-        token_words = keep.tile([P, T], I32, name="token_words", align_bytes=64)
+        token_words = keep.tile([P, WORD_WINDOW], I32, name="token_words", align_bytes=64)
         token_scales = keep.tile([P, BYTE_WINDOW], U8, name="token_scales", align_bytes=64)
         slot_words = keep.tile([P, SLOTS], U32, name="slot_words", align_bytes=64)
         slot_scales = keep.tile([P, SLOTS], U8, name="slot_scales", align_bytes=64)
@@ -57,12 +58,12 @@ def tile_moe_qkv_kernel(
         wq_s, wv_s = tiles("fp4_scales", 2, [P, E, N], U8)
         wk_raw = tiles("wk_raw", E, [P, PACK, N], F32)
         wk_bf = tiles("wk_bf", E, [P, N, PACK], BF16)
-        wk_w = tiles("wk_w", E, [P, N], U32)
         wk_s = tiles("wk_s", E, [P, N], U8)
-        y = tiles("y", BLOCKS, [P, SLOTS], F32)
+        y = {}
+        wk_w = {}
         gated = [tiles("gated%d_" % r, BLOCKS, [P, T], F32) for r in range(2)]
         result = tiles("result", BLOCKS, [P, T], F32)
-        turned_sum = {b: tiles("turned_sum%d_" % b, 2, [P, T // 2], F32) for b in (Q0, Q1, V0, V1)}
+        turned_sum = {}
         ident = keep.tile([P, P], F32, name="ident")
         warm = keep.tile([P, 8], F32, name="warm")
 
@@ -70,6 +71,7 @@ def tile_moe_qkv_kernel(
         nc.vector.memset(warm[:, 0:1], 0.0)
         nc.scalar.activation(warm[:, 4:5], warm[:, 0:1], IDENTITY)
         nc.vector.memset(token_scales[:, T:BYTE_WINDOW].bitcast(I32), 0)
+        nc.vector.memset(token_words[:, T:WORD_WINDOW], 0)
         for scales in (wq_s, wv_s):
             nc.vector.memset(scales[:].rearrange("p e n -> p (e n)").bitcast(I32), 0)
         make_identity(nc, ident[:])
@@ -88,20 +90,22 @@ def tile_moe_qkv_kernel(
         nc.sync.dma_start(offs_sb[:], offs)
         for i in range(4):
             nc.sync.dma_start(token_scales[i:P:QUADRANT, 0:T].bitcast(I32), x_scales[0, i::4, :].bitcast(I32))
-        nc.sync.dma_start(token_words[:], x_words[0].rearrange("p t d -> p (t d)").bitcast(I32))
         load_wk(0)
+        nc.sync.dma_start(token_words[:, 0:T], x_words[0].rearrange("p t d -> p (t d)").bitcast(I32))
         load_wk(1)
+        load_wk(2)
         load_fp4_scales(wq_s, wq_scales)
         load_fp4_words(wq_w, wq_words)
         nc.sync.dma_start(bias_sb[:, :, 0:E], bias.rearrange("(b p) e -> p b e", p=P))
-        for r, pos in enumerate((pos1, pos2)):
-            nc.sync.dma_start(pos_sb[r][:], pos)
-            nc.sync.dma_start(gate_sb[r][:], gate[r])
-        load_wk(2)
+        nc.sync.dma_start(pos_sb[0][:], pos1)
+        nc.sync.dma_start(gate_sb[0][:], gate[0])
+        nc.sync.dma_start(pos_sb[1][:], pos2)
+        nc.sync.dma_start(gate_sb[1][:], gate[1])
+        load_wk(3)
         load_fp4_scales(wv_s, wv_scales)
         load_fp4_words(wv_w, wv_words)
-        for e in range(3, E):
-            load_wk(e)
+        load_wk(4)
+        load_wk(5)
 
         def entries(list_sb, first, last):
             return list_sb[:, first // PER_COLUMN : last // PER_COLUMN]
@@ -113,56 +117,68 @@ def tile_moe_qkv_kernel(
 
         taken = []
 
-        def bank(width):
+        def bank(number, width):
             taken.append(width)
-            return psum.tile([P, width], F32, name="acc%d" % len(taken), tag="bank%d" % (len(taken) % BANKS))
+            return psum.tile([P, width], F32, name="acc%d" % len(taken), tag="bank%d" % number)
 
-        def quantise_wk(e):
+        def interleave_wk(e, copy, parts):
             src = wk_raw[e][:].rearrange("p j (c i) -> p c j i", i=4)
             dst = wk_bf[e][:].rearrange("p (c i) j -> p c j i", i=4)
-            for groups in (slice(0, N // 8), slice(N // 8, N // 4)):
-                nc.scalar.copy(dst[:, groups, :, :], src[:, groups, :, :])
+            step = N // 4 // parts
+            for first in range(0, N // 4, step):
+                copy(dst[:, first : first + step, :, :], src[:, first : first + step, :, :])
+
+        def quantise_wk(e, tag):
+            wk_w[e] = keep.tile([P, N], U32, name="wk_w%d" % e, tag=tag, align_bytes=64)
             nc.vector.quantize_mx(
                 out=wk_w[e][:].bitcast(FP8X4), scales=wk_s[e][:], in_=wk_bf[e][:].rearrange("p n j -> p (n j)")
             )
 
-        def pieces(experts, cuts):
-            borders = sorted(set(range(experts.start * C, experts.stop * C + 1, C)) | set(cuts))
-            return zip(borders[:-1], borders[1:])
-
-        def project(b, experts=range(E), cuts=()):
+        def project(b, banks, tag=None):
+            y[b] = keep.tile([P, SLOTS], F32, name="y%d" % b, tag=tag or "y%d" % b, align_bytes=64)
             cols = slice(b % 2 * P, (b % 2 + 1) * P)
-            for first, last in pieces(experts, cuts):
-                e = first // C
-                if b in (K0, K1):
-                    w, w_scale = wk_w[e][:, cols].bitcast(FP8X4), wk_s[e][:, cols]
-                else:
-                    words, scales = (wq_w, wq_s) if b in (Q0, Q1) else (wv_w, wv_s)
-                    w, w_scale = words[:, e, 2 * cols.start : 2 * cols.stop].bitcast(FP4X4), scales[:, e, cols]
-                slots = slice(first, last)
-                acc = bank(last - first)
-                nc.tensor.matmul_mx(
-                    out=acc[:],
-                    lhsT=w,
-                    lhsT_scale=w_scale,
-                    rhs=slot_words[:, slots].bitcast(FP8X4),
-                    rhs_scale=slot_scales[:, slots],
-                    start=True,
-                    stop=True,
-                )
-                nc.scalar.activation(y[b][:, slots], acc[:], IDENTITY, bias=bias_sb[:, b, e : e + 1])
+            doubles = E - len(banks)
+            for n, number in enumerate(banks):
+                first = n + min(n, doubles)
+                experts = range(first, first + (2 if n < doubles else 1))
+                acc = bank(number, len(experts) * C)
+                for i, e in enumerate(experts):
+                    if b in (K0, K1):
+                        w, w_scale = wk_w[e][:, cols].bitcast(FP8X4), wk_s[e][:, cols]
+                    else:
+                        words, scales = (wq_w, wq_s) if b in (Q0, Q1) else (wv_w, wv_s)
+                        w, w_scale = words[:, e, 2 * cols.start : 2 * cols.stop].bitcast(FP4X4), scales[:, e, cols]
+                    slots = slice(e * C, (e + 1) * C)
+                    nc.tensor.matmul_mx(
+                        out=acc[:, i * C : (i + 1) * C],
+                        lhsT=w,
+                        lhsT_scale=w_scale,
+                        rhs=slot_words[:, slots].bitcast(FP8X4),
+                        rhs_scale=slot_scales[:, slots],
+                        start=True,
+                        stop=True,
+                    )
+                for i, e in enumerate(experts):
+                    nc.scalar.activation(
+                        y[b][:, e * C : (e + 1) * C], acc[:, i * C : (i + 1) * C], IDENTITY, bias=bias_sb[:, b, e : e + 1]
+                    )
 
         def gather(r, b, tokens):
             picked = y[b][:].indirect(entries(pos_sb[r], tokens.start, tokens.stop))
             nc.vector.tensor_tensor(gated[r][b][:, tokens], picked, gate_sb[r][:, tokens], MULT)
 
         def gather_both(b):
-            gather(0, b, ALL)
-            gather(1, b, ALL)
+            if b == Q1:
+                gated[0][b] = keep.tile([P, T], F32, name="second", tag="y%d" % Q0, align_bytes=64)
+            for r in (1, 0) if b == Q1 else (0, 1):
+                gather(r, b, ALL)
 
-        def add_turned(b):
-            for h, tokens in enumerate(HALVES):
-                acc = bank(T // 2)
+        def add_turned(b, pair, halves=(0, 1), tag=None):
+            if b not in turned_sum:
+                turned_sum[b] = keep.tile([P, T], F32, name="turned_sum%d" % b, tag=tag or "turned_sum%d" % b, align_bytes=64)
+            for h in halves:
+                tokens = HALVES[h]
+                acc = bank(pair[h], T // 2)
                 for t in range(0, T // 2, P):
                     for r in range(2):
                         nc.tensor.matmul(
@@ -173,12 +189,12 @@ def tile_moe_qkv_kernel(
                             stop=(r == 1),
                             is_transpose=True,
                         )
-                nc.scalar.copy(turned_sum[b][h][:], acc[:])
+                nc.scalar.copy(turned_sum[b][:, tokens], acc[:])
 
-        def turn_back(b, h):
-            acc = bank(T // 2)
+        def turn_back(b, h, pair):
+            acc = bank(pair[h], T // 2)
             for t in range(0, T // 2, P):
-                nc.tensor.transpose(acc[:, t : t + P], turned_sum[b][h][:, t : t + P], ident[:])
+                nc.tensor.transpose(acc[:, t : t + P], turned_sum[b][:, HALVES[h].start + t : HALVES[h].start + t + P], ident[:])
             nc.scalar.copy(result[b][:, HALVES[h]], acc[:])
 
         def add(b, tokens):
@@ -187,47 +203,60 @@ def tile_moe_qkv_kernel(
         def store(queue, b, tokens):
             queue.dma_start(out[b * P : (b + 1) * P, tokens], result[b][:, tokens])
 
-        quantise_wk(0)
-        quantise_wk(1)
-        project(Q0, cuts=WORD_CUTS)
-        project(Q1)
-        quantise_wk(2)
-        project(V0)
-        project(V1, range(0, E // 2))
-        for e in range(3, E):
-            quantise_wk(e)
-        project(V1, range(E // 2, E))
-
+        interleave_wk(0, nc.scalar.copy, 2)
+        quantise_wk(0, "wk_w0")
+        interleave_wk(1, nc.scalar.copy, 2)
+        quantise_wk(1, "wk_w1")
+        interleave_wk(2, nc.scalar.copy, 2)
+        quantise_wk(2, "wk_w2")
+        project(Q0, (0, 1, 2, 3, 4, 5,))
+        project(Q1, (6, 7, 0,))
         gather_both(Q0)
         gather_both(Q1)
-        add_turned(Q0)
-        add_turned(Q1)
+        interleave_wk(3, nc.scalar.copy, 2)
+        quantise_wk(3, "wk_w3")
+        project(V0, (1, 2, 3, 7,))
+        interleave_wk(4, nc.scalar.copy, 2)
+        quantise_wk(4, "wk_w4")
+        interleave_wk(5, nc.scalar.copy, 2)
+        quantise_wk(5, "wk_w5")
         gather_both(V0)
-        project(K0)
-        for b in (Q0, Q1):
-            turn_back(b, 0)
-            turn_back(b, 1)
-            store(nc.sync, b, ALL)
+        add_turned(Q0, (1, 2,), tag="wk_raw5")
+        project(V1, (4, 5, 6,))
+        gated[0][V1] = keep.tile([P, T], F32, name="gated_late0V1", tag="wk_bf4", align_bytes=64)
+        gated[1][V1] = keep.tile([P, T], F32, name="gated_late1V1", tag="wk_bf5", align_bytes=64)
         gather_both(V1)
-        add_turned(V0)
-        project(K1)
-        turn_back(V0, 0)
-        turn_back(V0, 1)
-        store(nc.scalar, V0, ALL)
-        add_turned(V1)
-        for h, tokens in enumerate(HALVES):
-            turn_back(V1, h)
-            store(nc.scalar, V1, tokens)
-
-        gather(0, K0, ALL)
-        gather(1, K0, HEAD)
-        gather(1, K0, TAIL)
-        add(K0, HEAD)
-        add(K0, TAIL)
-        store(nc.sync, K0, ALL)
+        turn_back(Q0, 0, (0, 1,))
+        turn_back(Q0, 1, (0, 1,))
+        store(nc.sync, Q0, ALL)
+        add_turned(Q1, (3, 7,), tag="wk_raw4")
+        project(K0, (4, 5, 6,))
+        gather_both(K0)
+        add_turned(V0, (0, 1,))
+        turn_back(Q1, 0, (3, 7,))
+        turn_back(Q1, 1, (3, 7,))
+        store(nc.sync, Q1, ALL)
+        project(K1, (4, 5, 6,))
+        turn_back(V0, 0, (0, 1,))
+        turn_back(V0, 1, (0, 1,))
+        store(nc.sync, V0, ALL)
+        add_turned(V1, (3, 7,))
+        add_turned(K0, (0, 1,), (0,))
+        turn_back(V1, 0, (3, 7,))
+        store(nc.scalar, V1, HALVES[0])
+        turn_back(V1, 1, (3, 7,))
+        store(nc.scalar, V1, HALVES[1])
+        turn_back(K0, 0, (0, 1,))
+        store(nc.scalar, K0, HALVES[0])
         gather(0, K1, ALL)
         gather(1, K1, HEAD)
+        result[K0] = keep.tile([P, T], F32, name="late", tag="gate_sb0", align_bytes=64)
+        add(K0, HALVES[1])
+        store(nc.sync, K0, HALVES[1])
         gather(1, K1, TAIL)
-        for tokens in THIRDS:
-            add(K1, tokens)
-            store(nc.sync, K1, tokens)
+        add(K1, THIRDS[0])
+        store(nc.sync, K1, THIRDS[0])
+        add(K1, THIRDS[1])
+        store(nc.sync, K1, THIRDS[1])
+        add(K1, THIRDS[2])
+        store(nc.sync, K1, THIRDS[2])

@@ -29,7 +29,7 @@ BIAS_PITCH = 8
 QUADRANT = 32
 BYTE_WINDOW = 2048
 WORD_CUTS = (0, 512, 1024, 1280, SLOTS)
-WORD_WINDOW = 1024
+WORD_WINDOW = T
 HALVES = (slice(0, T // 2), slice(T // 2, T))
 HEAD, TAIL, ALL = slice(0, 512), slice(512, T), slice(0, T)
 THIRDS = tuple(slice(t, t + T // 3) for t in range(0, T, T // 3))
@@ -71,7 +71,6 @@ def tile_moe_qkv_kernel(
         nc.vector.memset(warm[:, 0:1], 0.0)
         nc.scalar.activation(warm[:, 4:5], warm[:, 0:1], IDENTITY)
         nc.vector.memset(token_scales[:, T:BYTE_WINDOW].bitcast(I32), 0)
-        nc.vector.memset(token_words[:, T:WORD_WINDOW], 0)
         for scales in (wq_s, wv_s):
             nc.vector.memset(scales[:].rearrange("p e n -> p (e n)").bitcast(I32), 0)
         make_identity(nc, ident[:])
@@ -93,12 +92,12 @@ def tile_moe_qkv_kernel(
         load_wk(0)
         nc.sync.dma_start(token_words[:, 0:T], x_words[0].rearrange("p t d -> p (t d)").bitcast(I32))
         load_wk(1)
-        load_wk(2)
         load_fp4_scales(wq_s, wq_scales)
         load_fp4_words(wq_w, wq_words)
         nc.sync.dma_start(bias_sb[:, :, 0:E], bias.rearrange("(b p) e -> p b e", p=P))
-        nc.sync.dma_start(pos_sb[0][:], pos1)
+        load_wk(2)
         nc.sync.dma_start(gate_sb[0][:], gate[0])
+        nc.sync.dma_start(pos_sb[0][:], pos1)
         nc.sync.dma_start(pos_sb[1][:], pos2)
         nc.sync.dma_start(gate_sb[1][:], gate[1])
         load_wk(3)
@@ -207,14 +206,14 @@ def tile_moe_qkv_kernel(
         quantise_wk(0, "wk_w0")
         interleave_wk(1, nc.scalar.copy, 2)
         quantise_wk(1, "wk_w1")
-        interleave_wk(2, nc.scalar.copy, 2)
-        quantise_wk(2, "wk_w2")
+        interleave_wk(2, nc.vector.tensor_copy, 1)
         project(Q0, (0, 1, 2, 3, 4, 5,))
         project(Q1, (6, 7, 0,))
         gather_both(Q0)
         gather_both(Q1)
         interleave_wk(3, nc.scalar.copy, 2)
         quantise_wk(3, "wk_w3")
+        quantise_wk(2, "y1")
         project(V0, (1, 2, 3, 7,))
         interleave_wk(4, nc.scalar.copy, 2)
         quantise_wk(4, "wk_w4")
@@ -231,7 +230,12 @@ def tile_moe_qkv_kernel(
         store(nc.sync, Q0, ALL)
         add_turned(Q1, (3, 7,), tag="wk_raw4")
         project(K0, (4, 5, 6,))
-        gather_both(K0)
+        gather(0, K0, ALL)
+        gather(1, K0, HEAD)
+        gather(1, K0, TAIL)
+        add(K0, HEAD)
+        add(K0, TAIL)
+        store(nc.sync, K0, ALL)
         add_turned(V0, (0, 1,))
         turn_back(Q1, 0, (3, 7,))
         turn_back(Q1, 1, (3, 7,))
@@ -241,18 +245,12 @@ def tile_moe_qkv_kernel(
         turn_back(V0, 1, (0, 1,))
         store(nc.sync, V0, ALL)
         add_turned(V1, (3, 7,))
-        add_turned(K0, (0, 1,), (0,))
         turn_back(V1, 0, (3, 7,))
         store(nc.scalar, V1, HALVES[0])
         turn_back(V1, 1, (3, 7,))
         store(nc.scalar, V1, HALVES[1])
-        turn_back(K0, 0, (0, 1,))
-        store(nc.scalar, K0, HALVES[0])
         gather(0, K1, ALL)
         gather(1, K1, HEAD)
-        result[K0] = keep.tile([P, T], F32, name="late", tag="gate_sb0", align_bytes=64)
-        add(K0, HALVES[1])
-        store(nc.sync, K0, HALVES[1])
         gather(1, K1, TAIL)
         add(K1, THIRDS[0])
         store(nc.sync, K1, THIRDS[0])

@@ -28,7 +28,7 @@ RING = 5
 BIAS_PITCH = 8
 QUADRANT = 32
 BYTE_WINDOW = 2048
-WORD_CUTS = (0, 512, 1024, 1280, SLOTS)
+WORD_CUTS = (0, 512, 1024, 1280, 1408, SLOTS)
 WORD_WINDOW = T
 HALVES = (slice(0, T // 2), slice(T // 2, T))
 HEAD, TAIL, ALL = slice(0, 512), slice(512, T), slice(0, T)
@@ -120,12 +120,10 @@ def tile_moe_qkv_kernel(
             taken.append(width)
             return psum.tile([P, width], F32, name="acc%d" % len(taken), tag="bank%d" % number)
 
-        def interleave_wk(e, copy, parts):
+        def interleave_wk(e, copy, first, last):
             src = wk_raw[e][:].rearrange("p j (c i) -> p c j i", i=4)
             dst = wk_bf[e][:].rearrange("p (c i) j -> p c j i", i=4)
-            step = N // 4 // parts
-            for first in range(0, N // 4, step):
-                copy(dst[:, first : first + step, :, :], src[:, first : first + step, :, :])
+            copy(dst[:, first // 4 : last // 4, :, :], src[:, first // 4 : last // 4, :, :])
 
         def quantise_wk(e, tag):
             wk_w[e] = keep.tile([P, N], U32, name="wk_w%d" % e, tag=tag, align_bytes=64)
@@ -133,23 +131,26 @@ def tile_moe_qkv_kernel(
                 out=wk_w[e][:].bitcast(FP8X4), scales=wk_s[e][:], in_=wk_bf[e][:].rearrange("p n j -> p (n j)")
             )
 
-        def project(b, banks, tag=None):
+        def project(b, banks, tag=None, cuts=()):
             y[b] = keep.tile([P, SLOTS], F32, name="y%d" % b, tag=tag or "y%d" % b, align_bytes=64)
             cols = slice(b % 2 * P, (b % 2 + 1) * P)
-            doubles = E - len(banks)
+            borders = sorted(set(range(0, SLOTS + 1, C)) | set(cuts))
+            pieces = [slice(first, last) for first, last in zip(borders[:-1], borders[1:])]
+            doubles = len(pieces) - len(banks)
             for n, number in enumerate(banks):
                 first = n + min(n, doubles)
-                experts = range(first, first + (2 if n < doubles else 1))
-                acc = bank(number, len(experts) * C)
-                for i, e in enumerate(experts):
+                group = pieces[first : first + (2 if n < doubles else 1)]
+                acc = bank(number, group[-1].stop - group[0].start)
+                parts = [acc[:, slots.start - group[0].start : slots.stop - group[0].start] for slots in group]
+                for slots, part in zip(group, parts):
+                    e = slots.start // C
                     if b in (K0, K1):
                         w, w_scale = wk_w[e][:, cols].bitcast(FP8X4), wk_s[e][:, cols]
                     else:
                         words, scales = (wq_w, wq_s) if b in (Q0, Q1) else (wv_w, wv_s)
                         w, w_scale = words[:, e, 2 * cols.start : 2 * cols.stop].bitcast(FP4X4), scales[:, e, cols]
-                    slots = slice(e * C, (e + 1) * C)
                     nc.tensor.matmul_mx(
-                        out=acc[:, i * C : (i + 1) * C],
+                        out=part,
                         lhsT=w,
                         lhsT_scale=w_scale,
                         rhs=slot_words[:, slots].bitcast(FP8X4),
@@ -157,10 +158,9 @@ def tile_moe_qkv_kernel(
                         start=True,
                         stop=True,
                     )
-                for i, e in enumerate(experts):
-                    nc.scalar.activation(
-                        y[b][:, e * C : (e + 1) * C], acc[:, i * C : (i + 1) * C], IDENTITY, bias=bias_sb[:, b, e : e + 1]
-                    )
+                for slots, part in zip(group, parts):
+                    e = slots.start // C
+                    nc.scalar.activation(y[b][:, slots], part, IDENTITY, bias=bias_sb[:, b, e : e + 1])
 
         def gather(r, b, tokens):
             picked = y[b][:].indirect(entries(pos_sb[r], tokens.start, tokens.stop))
@@ -202,22 +202,28 @@ def tile_moe_qkv_kernel(
         def store(queue, b, tokens):
             queue.dma_start(out[b * P : (b + 1) * P, tokens], result[b][:, tokens])
 
-        interleave_wk(0, nc.scalar.copy, 2)
+        interleave_wk(0, nc.scalar.copy, 0, N // 2)
+        interleave_wk(0, nc.scalar.copy, N // 2, N)
         quantise_wk(0, "wk_w0")
-        interleave_wk(1, nc.scalar.copy, 2)
+        interleave_wk(1, nc.scalar.copy, 0, N // 2)
+        interleave_wk(1, nc.scalar.copy, N // 2, N)
         quantise_wk(1, "wk_w1")
-        interleave_wk(2, nc.vector.tensor_copy, 1)
-        project(Q0, (0, 1, 2, 3, 4, 5,))
-        project(Q1, (6, 7, 0,))
+        interleave_wk(2, nc.vector.tensor_copy, 0, 128)
+        project(Q0, (0, 1, 2, 3, 4, 5, 6), cuts=WORD_CUTS)
+        project(Q1, (7, 0, 1))
         gather_both(Q0)
         gather_both(Q1)
-        interleave_wk(3, nc.scalar.copy, 2)
+        interleave_wk(2, nc.scalar.copy, 128, N)
+        interleave_wk(3, nc.scalar.copy, 0, N // 2)
+        interleave_wk(3, nc.scalar.copy, N // 2, N)
         quantise_wk(3, "wk_w3")
         quantise_wk(2, "y1")
         project(V0, (1, 2, 3, 7,))
-        interleave_wk(4, nc.scalar.copy, 2)
+        interleave_wk(4, nc.scalar.copy, 0, N // 2)
+        interleave_wk(4, nc.scalar.copy, N // 2, N)
         quantise_wk(4, "wk_w4")
-        interleave_wk(5, nc.scalar.copy, 2)
+        interleave_wk(5, nc.scalar.copy, 0, N // 2)
+        interleave_wk(5, nc.scalar.copy, N // 2, N)
         quantise_wk(5, "wk_w5")
         gather_both(V0)
         add_turned(Q0, (1, 2,), tag="wk_raw5")
@@ -231,11 +237,10 @@ def tile_moe_qkv_kernel(
         add_turned(Q1, (3, 7,), tag="wk_raw4")
         project(K0, (4, 5, 6,))
         gather(0, K0, ALL)
-        gather(1, K0, HEAD)
-        gather(1, K0, TAIL)
-        add(K0, HEAD)
-        add(K0, TAIL)
-        store(nc.sync, K0, ALL)
+        gather(1, K0, HALVES[1])
+        gather(1, K0, HALVES[0])
+        add(K0, HALVES[1])
+        store(nc.sync, K0, HALVES[1])
         add_turned(V0, (0, 1,))
         turn_back(Q1, 0, (3, 7,))
         turn_back(Q1, 1, (3, 7,))
@@ -245,10 +250,13 @@ def tile_moe_qkv_kernel(
         turn_back(V0, 1, (0, 1,))
         store(nc.sync, V0, ALL)
         add_turned(V1, (3, 7,))
+        add_turned(K0, (0, 1,), (0,))
         turn_back(V1, 0, (3, 7,))
         store(nc.scalar, V1, HALVES[0])
         turn_back(V1, 1, (3, 7,))
         store(nc.scalar, V1, HALVES[1])
+        turn_back(K0, 0, (0, 1,))
+        store(nc.scalar, K0, HALVES[0])
         gather(0, K1, ALL)
         gather(1, K1, HEAD)
         gather(1, K1, TAIL)

@@ -101,8 +101,8 @@ def tile_moe_qkv_kernel(
         nc.sync.dma_start(pos_sb[1][:], pos2)
         nc.sync.dma_start(gate_sb[1][:], gate[1])
         load_wk(3)
-        load_fp4_scales(wv_s, wv_scales)
         load_fp4_words(wv_w, wv_words)
+        load_fp4_scales(wv_s, wv_scales)
         load_wk(4)
         load_wk(5)
 
@@ -172,13 +172,13 @@ def tile_moe_qkv_kernel(
             for r in (1, 0) if b == Q1 else (0, 1):
                 gather(r, b, ALL)
 
-        def add_turned(b, pair, halves=(0, 1), tag=None):
+        def add_turned(b, pair, halves=(0, 1), tag=None, parts=HALVES):
             if b not in turned_sum:
                 turned_sum[b] = keep.tile([P, T], F32, name="turned_sum%d" % b, tag=tag or "turned_sum%d" % b, align_bytes=64)
             for h in halves:
-                tokens = HALVES[h]
-                acc = bank(pair[h], T // 2)
-                for t in range(0, T // 2, P):
+                tokens = parts[h]
+                acc = bank(pair[h], tokens.stop - tokens.start)
+                for t in range(0, tokens.stop - tokens.start, P):
                     for r in range(2):
                         nc.tensor.matmul(
                             acc[:, t : t + P],
@@ -190,11 +190,12 @@ def tile_moe_qkv_kernel(
                         )
                 nc.scalar.copy(turned_sum[b][:, tokens], acc[:])
 
-        def turn_back(b, h, pair):
-            acc = bank(pair[h], T // 2)
-            for t in range(0, T // 2, P):
-                nc.tensor.transpose(acc[:, t : t + P], turned_sum[b][:, HALVES[h].start + t : HALVES[h].start + t + P], ident[:])
-            nc.scalar.copy(result[b][:, HALVES[h]], acc[:])
+        def turn_back(b, h, pair, parts=HALVES):
+            tokens = parts[h]
+            acc = bank(pair[h], tokens.stop - tokens.start)
+            for t in range(0, tokens.stop - tokens.start, P):
+                nc.tensor.transpose(acc[:, t : t + P], turned_sum[b][:, tokens.start + t : tokens.start + t + P], ident[:])
+            nc.scalar.copy(result[b][:, tokens], acc[:])
 
         def add(b, tokens):
             nc.vector.tensor_tensor(result[b][:, tokens], gated[0][b][:, tokens], gated[1][b][:, tokens], ADD)
@@ -208,22 +209,18 @@ def tile_moe_qkv_kernel(
         interleave_wk(1, nc.scalar.copy, 0, N // 2)
         interleave_wk(1, nc.scalar.copy, N // 2, N)
         quantise_wk(1, "wk_w1")
-        interleave_wk(2, nc.vector.tensor_copy, 0, 128)
+        interleave_wk(2, nc.vector.tensor_copy, 0, 256)
         project(Q0, (0, 1, 2, 3, 4, 5, 6), cuts=WORD_CUTS)
-        project(Q1, (7, 0, 1))
+        project(Q1, (7, 0, 1, 2, 3, 4))
         gather_both(Q0)
         gather_both(Q1)
-        interleave_wk(2, nc.scalar.copy, 128, N)
-        interleave_wk(3, nc.scalar.copy, 0, N // 2)
-        interleave_wk(3, nc.scalar.copy, N // 2, N)
+        interleave_wk(3, nc.scalar.copy, 0, N)
         quantise_wk(3, "wk_w3")
         quantise_wk(2, "y1")
         project(V0, (1, 2, 3, 7,))
-        interleave_wk(4, nc.scalar.copy, 0, N // 2)
-        interleave_wk(4, nc.scalar.copy, N // 2, N)
+        interleave_wk(4, nc.scalar.copy, 0, N)
         quantise_wk(4, "wk_w4")
-        interleave_wk(5, nc.scalar.copy, 0, N // 2)
-        interleave_wk(5, nc.scalar.copy, N // 2, N)
+        interleave_wk(5, nc.scalar.copy, 0, N)
         quantise_wk(5, "wk_w5")
         gather_both(V0)
         add_turned(Q0, (1, 2,), tag="wk_raw5")
@@ -237,10 +234,8 @@ def tile_moe_qkv_kernel(
         add_turned(Q1, (3, 7,), tag="wk_raw4")
         project(K0, (4, 5, 6,))
         gather(0, K0, ALL)
-        gather(1, K0, HALVES[1])
-        gather(1, K0, HALVES[0])
-        add(K0, HALVES[1])
-        store(nc.sync, K0, HALVES[1])
+        for tokens in THIRDS:
+            gather(1, K0, tokens)
         add_turned(V0, (0, 1,))
         turn_back(Q1, 0, (3, 7,))
         turn_back(Q1, 1, (3, 7,))
@@ -250,13 +245,15 @@ def tile_moe_qkv_kernel(
         turn_back(V0, 1, (0, 1,))
         store(nc.sync, V0, ALL)
         add_turned(V1, (3, 7,))
-        add_turned(K0, (0, 1,), (0,))
+        add_turned(K0, (4, 5, 6), (0, 1, 2), parts=THIRDS)
         turn_back(V1, 0, (3, 7,))
-        store(nc.scalar, V1, HALVES[0])
+        store(nc.sync, V1, HALVES[0])
         turn_back(V1, 1, (3, 7,))
-        store(nc.scalar, V1, HALVES[1])
-        turn_back(K0, 0, (0, 1,))
-        store(nc.scalar, K0, HALVES[0])
+        store(nc.sync, V1, HALVES[1])
+        for h, tokens in enumerate(THIRDS):
+            turn_back(K0, h, (4, 5, 6), parts=THIRDS)
+            store(nc.sync, K0, tokens)
+        result[K1] = keep.tile([P, T], F32, name="last", tag="turned_sum%d" % K0, align_bytes=64)
         gather(0, K1, ALL)
         gather(1, K1, HEAD)
         gather(1, K1, TAIL)

@@ -49,8 +49,9 @@ def tile_moe_qkv_kernel(
         offs_sb = keep.tile([P, SLOTS // PER_COLUMN], U16, name="offs_sb")
         pos_sb = tiles("pos_sb", 2, [P, T // PER_COLUMN], U16)
         gate_sb = tiles("gate_sb", 2, [P, T], F32)
-        bias_sb = keep.tile([P, BLOCKS, BIAS_PITCH], F32, name="bias_sb")
-        token_words = keep.tile([P, WORD_WINDOW], I32, name="token_words", align_bytes=64)
+        bias_q = keep.tile([P, 2, BIAS_PITCH], F32, name="bias_q")
+        bias_kv = keep.tile([P, BLOCKS - 2, BIAS_PITCH], F32, name="bias_kv")
+        token_words = keep.tile([P, WORD_WINDOW], I32, name="token_words", tag="token_words", align_bytes=64)
         token_scales = keep.tile([P, BYTE_WINDOW], U8, name="token_scales", align_bytes=64)
         slot_words = keep.tile([P, SLOTS], U32, name="slot_words", align_bytes=64)
         slot_scales = keep.tile([P, SLOTS], U8, name="slot_scales", align_bytes=64)
@@ -83,8 +84,8 @@ def tile_moe_qkv_kernel(
                 rows = src[:, 0, i::4, :].rearrange("e q n -> q e n")
                 nc.sync.dma_start(dst[i:P:QUADRANT, :, :].bitcast(I32), rows.bitcast(I32))
 
-        def load_wk(e):
-            nc.sync.dma_start(wk_raw[e][:], wk[e].rearrange("(p j) n -> p j n", j=PACK))
+        def load_wk(e, queue=nc.sync):
+            queue.dma_start(wk_raw[e][:], wk[e].rearrange("(p j) n -> p j n", j=PACK))
 
         nc.sync.dma_start(offs_sb[:], offs)
         for i in range(4):
@@ -94,12 +95,13 @@ def tile_moe_qkv_kernel(
         load_wk(1)
         load_fp4_scales(wq_s, wq_scales)
         load_fp4_words(wq_w, wq_words)
-        nc.sync.dma_start(bias_sb[:, :, 0:E], bias.rearrange("(b p) e -> p b e", p=P))
+        nc.sync.dma_start(bias_q[:, :, 0:E], bias[0:N].rearrange("(b p) e -> p b e", p=P))
         load_wk(2)
         nc.sync.dma_start(gate_sb[0][:], gate[0])
         nc.sync.dma_start(pos_sb[0][:], pos1)
         nc.sync.dma_start(pos_sb[1][:], pos2)
         nc.sync.dma_start(gate_sb[1][:], gate[1])
+        nc.sync.dma_start(bias_kv[:, :, 0:E], bias[N : 3 * N].rearrange("(b p) e -> p b e", p=P))
         load_wk(3)
         load_fp4_words(wv_w, wv_words)
         load_fp4_scales(wv_s, wv_scales)
@@ -126,9 +128,10 @@ def tile_moe_qkv_kernel(
             copy(dst[:, first // 4 : last // 4, :, :], src[:, first // 4 : last // 4, :, :])
 
         def quantise_wk(e, tag):
-            wk_w[e] = keep.tile([P, N], U32, name="wk_w%d" % e, tag=tag, align_bytes=64)
+            if e not in wk_w:
+                wk_w[e] = keep.tile([P, N], U32, name="wk_w%d" % e, tag=tag, align_bytes=64)[:]
             nc.vector.quantize_mx(
-                out=wk_w[e][:].bitcast(FP8X4), scales=wk_s[e][:], in_=wk_bf[e][:].rearrange("p n j -> p (n j)")
+                out=wk_w[e].bitcast(FP8X4), scales=wk_s[e][:], in_=wk_bf[e][:].rearrange("p n j -> p (n j)")
             )
 
         def project(b, banks, tag=None, cuts=()):
@@ -160,7 +163,7 @@ def tile_moe_qkv_kernel(
                     )
                 for slots, part in zip(group, parts):
                     e = slots.start // C
-                    nc.scalar.activation(y[b][:, slots], part, IDENTITY, bias=bias_sb[:, b, e : e + 1])
+                    nc.scalar.activation(y[b][:, slots], part, IDENTITY, bias=(bias_q[:, b, e : e + 1] if b < 2 else bias_kv[:, b - 2, e : e + 1]))
 
         def gather(r, b, tokens):
             picked = y[b][:].indirect(entries(pos_sb[r], tokens.start, tokens.stop))
@@ -205,18 +208,21 @@ def tile_moe_qkv_kernel(
 
         interleave_wk(0, nc.scalar.copy, 0, N // 2)
         interleave_wk(0, nc.scalar.copy, N // 2, N)
-        quantise_wk(0, "wk_w0")
+        early = keep.tile([P, 3, N], U32, name="early", tag="token_words", align_bytes=64)
+        for e in range(3):
+            wk_w[e] = early[:, e, :]
+        quantise_wk(0, None)
         interleave_wk(1, nc.scalar.copy, 0, N // 2)
         interleave_wk(1, nc.scalar.copy, N // 2, N)
-        quantise_wk(1, "wk_w1")
-        interleave_wk(2, nc.vector.tensor_copy, 0, 256)
+        quantise_wk(1, None)
+        nc.gpsimd.tensor_scalar(wk_bf[2][:], wk_raw[2][:].rearrange("p j n -> p n j"), 1.0, 0.0, MULT, ADD)
+        quantise_wk(2, None)
         project(Q0, (0, 1, 2, 3, 4, 5, 6), cuts=WORD_CUTS)
         project(Q1, (7, 0, 1, 2, 3, 4))
         gather_both(Q0)
         gather_both(Q1)
         interleave_wk(3, nc.scalar.copy, 0, N)
         quantise_wk(3, "wk_w3")
-        quantise_wk(2, "y1")
         project(V0, (1, 2, 3, 7,))
         interleave_wk(4, nc.scalar.copy, 0, N)
         quantise_wk(4, "wk_w4")

@@ -88,9 +88,10 @@ def tile_moe_qkv_kernel(
             queue.dma_start(wk_raw[e][:], wk[e].rearrange("(p j) n -> p j n", j=PACK))
 
         nc.sync.dma_start(offs_sb[:], offs)
+        nc.sync.dma_start(wk_raw[0][:, 0:2, :], wk[0].rearrange("(p j) n -> p j n", j=PACK)[:, 0:2, :])
         for i in range(4):
             nc.sync.dma_start(token_scales[i:P:QUADRANT, 0:T].bitcast(I32), x_scales[0, i::4, :].bitcast(I32))
-        load_wk(0)
+        nc.sync.dma_start(wk_raw[0][:, 2:4, :], wk[0].rearrange("(p j) n -> p j n", j=PACK)[:, 2:4, :])
         nc.sync.dma_start(token_words[:, 0:T], x_words[0].rearrange("p t d -> p (t d)").bitcast(I32))
         load_wk(1)
         load_fp4_scales(wq_s, wq_scales)

@@ -18,21 +18,24 @@ FP4X4 = mybir.dt.float4_e2m1fn_x4
 MULT = mybir.AluOpType.mult
 ADD = mybir.AluOpType.add
 IDENTITY = mybir.ActivationFunctionType.Identity
+COPY = mybir.ActivationFunctionType.Copy
 
 P = 128
 PACK = 4
 PER_COLUMN = 16
 BLOCKS = 3 * N // P
 Q0, Q1, K0, K1, V0, V1 = range(BLOCKS)
-RING = 5
 BIAS_PITCH = 8
 QUADRANT = 32
+BANK = 512
 BYTE_WINDOW = 2048
-WORD_CUTS = (0, 512, 1024, 1280, 1408, SLOTS)
-WORD_WINDOW = T
-HALVES = (slice(0, T // 2), slice(T // 2, T))
+WORD_CUTS = (0, 256, 512, 1024, SLOTS)
 HEAD, TAIL, ALL = slice(0, 512), slice(512, T), slice(0, T)
 THIRDS = tuple(slice(t, t + T // 3) for t in range(0, T, T // 3))
+TOKEN_TILES = T // P
+TURNS = ((0, 2), (2, 4), (4, 5), (5, 6))
+LAST = (slice(0, 384), slice(384, 640), slice(640, T))
+EARLY = 3
 
 
 def tile_moe_qkv_kernel(
@@ -43,30 +46,32 @@ def tile_moe_qkv_kernel(
         keep = ctx.enter_context(tc.tile_pool(name="keep", bufs=1))
         psum = ctx.enter_context(tc.psum_pool(name="psum", bufs=1))
 
+        def tile(name, shape, dtype, tag=None):
+            return keep.tile(shape, dtype, name=name, tag=tag or name, align_bytes=64)
+
         def tiles(name, count, shape, dtype):
-            return [keep.tile(shape, dtype, name="%s%d" % (name, i), align_bytes=64) for i in range(count)]
+            return [tile("%s%d" % (name, i), shape, dtype) for i in range(count)]
 
         offs_sb = keep.tile([P, SLOTS // PER_COLUMN], U16, name="offs_sb")
         pos_sb = tiles("pos_sb", 2, [P, T // PER_COLUMN], U16)
         gate_sb = tiles("gate_sb", 2, [P, T], F32)
-        bias_q = keep.tile([P, 2, BIAS_PITCH], F32, name="bias_q")
-        bias_kv = keep.tile([P, BLOCKS - 2, BIAS_PITCH], F32, name="bias_kv")
-        token_words = keep.tile([P, WORD_WINDOW], I32, name="token_words", tag="token_words", align_bytes=64)
-        token_scales = keep.tile([P, BYTE_WINDOW], U8, name="token_scales", align_bytes=64)
-        slot_words = keep.tile([P, SLOTS], U32, name="slot_words", align_bytes=64)
-        slot_scales = keep.tile([P, SLOTS], U8, name="slot_scales", align_bytes=64)
+        gate_col = tile("gate_col", [P, 2 * TOKEN_TILES], F32)
+        bias_q = tile("bias_q", [P, 2, BIAS_PITCH], F32)
+        bias_kv = tile("bias_kv", [P, BLOCKS - 2, BIAS_PITCH], F32)
+        token_words = tile("token_words", [P, T], I32)
+        token_scales = tile("token_scales", [P, BYTE_WINDOW], U8)
+        slot_words = tile("slot_words", [P, SLOTS], U32)
+        slot_scales = tile("slot_scales", [P, SLOTS], U8)
         wq_w, wv_w = tiles("fp4_words", 2, [P, E, 2 * N], U8)
         wq_s, wv_s = tiles("fp4_scales", 2, [P, E, N], U8)
-        wk_raw = tiles("wk_raw", E, [P, PACK, N], F32)
+        wk_early = tiles("wk_early", E, [P, PACK, N], F32)
+        wk_raw = [t[:] for t in wk_early]
         wk_bf = tiles("wk_bf", E, [P, N, PACK], BF16)
         wk_s = tiles("wk_s", E, [P, N], U8)
-        y = {}
         wk_w = {}
-        gated = [tiles("gated%d_" % r, BLOCKS, [P, T], F32) for r in range(2)]
-        result = tiles("result", BLOCKS, [P, T], F32)
-        turned_sum = {}
-        ident = keep.tile([P, P], F32, name="ident")
-        warm = keep.tile([P, 8], F32, name="warm")
+        y = tiles("y", BLOCKS, [P, SLOTS], F32)
+        ident = tile("ident", [P, P], F32)
+        warm = tile("warm", [P, 8], F32)
 
         nc.gpsimd.memset(token_scales[:, 0:T].bitcast(I32), 0)
         nc.vector.memset(warm[:, 0:1], 0.0)
@@ -84,30 +89,30 @@ def tile_moe_qkv_kernel(
                 rows = src[:, 0, i::4, :].rearrange("e q n -> q e n")
                 nc.sync.dma_start(dst[i:P:QUADRANT, :, :].bitcast(I32), rows.bitcast(I32))
 
-        def load_wk(e, queue=nc.sync):
-            queue.dma_start(wk_raw[e][:], wk[e].rearrange("(p j) n -> p j n", j=PACK))
+        def wk_rows(e):
+            return wk[e].rearrange("(p j) n -> p j n", j=PACK)
 
         nc.sync.dma_start(offs_sb[:], offs)
-        nc.sync.dma_start(wk_raw[0][:, 0:2, :], wk[0].rearrange("(p j) n -> p j n", j=PACK)[:, 0:2, :])
+        nc.sync.dma_start(wk_early[0][:, 0:2, :], wk_rows(0)[:, 0:2, :])
         for i in range(4):
             nc.sync.dma_start(token_scales[i:P:QUADRANT, 0:T].bitcast(I32), x_scales[0, i::4, :].bitcast(I32))
-        nc.sync.dma_start(wk_raw[0][:, 2:4, :], wk[0].rearrange("(p j) n -> p j n", j=PACK)[:, 2:4, :])
-        nc.sync.dma_start(token_words[:, 0:T], x_words[0].rearrange("p t d -> p (t d)").bitcast(I32))
-        load_wk(1)
+        nc.sync.dma_start(wk_early[0][:, 2:4, :], wk_rows(0)[:, 2:4, :])
+        nc.sync.dma_start(token_words[:], x_words[0].rearrange("p t d -> p (t d)").bitcast(I32))
+        nc.sync.dma_start(wk_early[1][:], wk_rows(1))
         load_fp4_scales(wq_s, wq_scales)
         load_fp4_words(wq_w, wq_words)
         nc.sync.dma_start(bias_q[:, :, 0:E], bias[0:N].rearrange("(b p) e -> p b e", p=P))
-        load_wk(2)
+        nc.sync.dma_start(wk_early[2][:], wk_rows(2))
+        load_fp4_words(wv_w, wv_words)
+        nc.sync.dma_start(wk_early[3][:], wk_rows(3))
+        load_fp4_scales(wv_s, wv_scales)
+        nc.sync.dma_start(bias_kv[:, :, 0:E], bias[N : 3 * N].rearrange("(b p) e -> p b e", p=P))
+        nc.sync.dma_start(wk_early[4][:], wk_rows(4))
+        nc.sync.dma_start(wk_early[5][:], wk_rows(5))
         nc.sync.dma_start(gate_sb[0][:], gate[0])
         nc.sync.dma_start(pos_sb[0][:], pos1)
-        nc.sync.dma_start(pos_sb[1][:], pos2)
         nc.sync.dma_start(gate_sb[1][:], gate[1])
-        nc.sync.dma_start(bias_kv[:, :, 0:E], bias[N : 3 * N].rearrange("(b p) e -> p b e", p=P))
-        load_wk(3)
-        load_fp4_words(wv_w, wv_words)
-        load_fp4_scales(wv_s, wv_scales)
-        load_wk(4)
-        load_wk(5)
+        nc.sync.dma_start(pos_sb[1][:], pos2)
 
         def entries(list_sb, first, last):
             return list_sb[:, first // PER_COLUMN : last // PER_COLUMN]
@@ -119,154 +124,183 @@ def tile_moe_qkv_kernel(
 
         taken = []
 
-        def bank(number, width):
+        def bank(number, width=BANK):
             taken.append(width)
             return psum.tile([P, width], F32, name="acc%d" % len(taken), tag="bank%d" % number)
 
-        def interleave_wk(e, copy, first, last):
-            src = wk_raw[e][:].rearrange("p j (c i) -> p c j i", i=4)
+        def interleave_wk(e, copy, first=0, last=N):
+            src = wk_raw[e].rearrange("p j (c i) -> p c j i", i=4)
             dst = wk_bf[e][:].rearrange("p (c i) j -> p c j i", i=4)
             copy(dst[:, first // 4 : last // 4, :, :], src[:, first // 4 : last // 4, :, :])
 
-        def quantise_wk(e, tag):
+        def quantise_wk(e):
             if e not in wk_w:
-                wk_w[e] = keep.tile([P, N], U32, name="wk_w%d" % e, tag=tag, align_bytes=64)[:]
+                wk_w[e] = tile("wk_w%d" % e, [P, N], U32)[:]
             nc.vector.quantize_mx(
                 out=wk_w[e].bitcast(FP8X4), scales=wk_s[e][:], in_=wk_bf[e][:].rearrange("p n j -> p (n j)")
             )
 
-        def project(b, banks, tag=None, cuts=()):
-            y[b] = keep.tile([P, SLOTS], F32, name="y%d" % b, tag=tag or "y%d" % b, align_bytes=64)
-            cols = slice(b % 2 * P, (b % 2 + 1) * P)
-            borders = sorted(set(range(0, SLOTS + 1, C)) | set(cuts))
-            pieces = [slice(first, last) for first, last in zip(borders[:-1], borders[1:])]
-            doubles = len(pieces) - len(banks)
-            for n, number in enumerate(banks):
-                first = n + min(n, doubles)
-                group = pieces[first : first + (2 if n < doubles else 1)]
-                acc = bank(number, group[-1].stop - group[0].start)
-                parts = [acc[:, slots.start - group[0].start : slots.stop - group[0].start] for slots in group]
-                for slots, part in zip(group, parts):
-                    e = slots.start // C
-                    if b in (K0, K1):
-                        w, w_scale = wk_w[e][:, cols].bitcast(FP8X4), wk_s[e][:, cols]
-                    else:
-                        words, scales = (wq_w, wq_s) if b in (Q0, Q1) else (wv_w, wv_s)
-                        w, w_scale = words[:, e, 2 * cols.start : 2 * cols.stop].bitcast(FP4X4), scales[:, e, cols]
-                    nc.tensor.matmul_mx(
-                        out=part,
-                        lhsT=w,
-                        lhsT_scale=w_scale,
-                        rhs=slot_words[:, slots].bitcast(FP8X4),
-                        rhs_scale=slot_scales[:, slots],
-                        start=True,
-                        stop=True,
-                    )
-                for slots, part in zip(group, parts):
-                    e = slots.start // C
-                    nc.scalar.activation(y[b][:, slots], part, IDENTITY, bias=(bias_q[:, b, e : e + 1] if b < 2 else bias_kv[:, b - 2, e : e + 1]))
+        def project(number, pieces):
+            acc = bank(number, sum(s.stop - s.start for b, s in pieces))
+            at = 0
+            parts = []
+            for b, slots in pieces:
+                part = acc[:, at : at + slots.stop - slots.start]
+                at = at + slots.stop - slots.start
+                parts.append(part)
+                e = slots.start // C
+                cols = slice(b % 2 * P, (b % 2 + 1) * P)
+                if b in (K0, K1):
+                    w, w_scale = wk_w[e][:, cols].bitcast(FP8X4), wk_s[e][:, cols]
+                else:
+                    words, scales = (wq_w, wq_s) if b in (Q0, Q1) else (wv_w, wv_s)
+                    w, w_scale = words[:, e, 2 * cols.start : 2 * cols.stop].bitcast(FP4X4), scales[:, e, cols]
+                nc.tensor.matmul_mx(
+                    out=part,
+                    lhsT=w,
+                    lhsT_scale=w_scale,
+                    rhs=slot_words[:, slots].bitcast(FP8X4),
+                    rhs_scale=slot_scales[:, slots],
+                    start=True,
+                    stop=True,
+                )
+            for (b, slots), part in zip(pieces, parts):
+                e = slots.start // C
+                column = bias_q[:, b, e : e + 1] if b < 2 else bias_kv[:, b - 2, e : e + 1]
+                nc.scalar.activation(y[b][:, slots], part, IDENTITY, bias=column)
 
-        def gather(r, b, tokens):
+        def expert(e):
+            return slice(e * C, (e + 1) * C)
+
+        def project_block(b, banks):
+            for pair in range(E // 2):
+                project(banks[pair % len(banks)], [(b, expert(2 * pair)), (b, expert(2 * pair + 1))])
+
+        gated = {}
+        result = {}
+
+        def gather(r, b, tokens, tag=None):
+            if (r, b) not in gated:
+                gated[r, b] = tile("gated%d_%d" % (r, b), [P, T], F32, tag)
             picked = y[b][:].indirect(entries(pos_sb[r], tokens.start, tokens.stop))
-            nc.vector.tensor_tensor(gated[r][b][:, tokens], picked, gate_sb[r][:, tokens], MULT)
+            nc.vector.tensor_tensor(gated[r, b][:, tokens], picked, gate_sb[r][:, tokens], MULT)
 
-        def gather_both(b):
-            if b == Q1:
-                gated[0][b] = keep.tile([P, T], F32, name="second", tag="y%d" % Q0, align_bytes=64)
-            for r in (1, 0) if b == Q1 else (0, 1):
-                gather(r, b, ALL)
+        def add_and_store(b, tokens, tag=None):
+            if b not in result:
+                result[b] = tile("result%d" % b, [P, T], F32, tag)
+            nc.vector.tensor_tensor(result[b][:, tokens], gated[0, b][:, tokens], gated[1, b][:, tokens], ADD)
+            nc.sync.dma_start(out[b * P : (b + 1) * P, tokens], result[b][:, tokens])
 
-        def add_turned(b, pair, halves=(0, 1), tag=None, parts=HALVES):
-            if b not in turned_sum:
-                turned_sum[b] = keep.tile([P, T], F32, name="turned_sum%d" % b, tag=tag or "turned_sum%d" % b, align_bytes=64)
-            for h in halves:
-                tokens = parts[h]
-                acc = bank(pair[h], tokens.stop - tokens.start)
-                for t in range(0, tokens.stop - tokens.start, P):
+        def combine(b, pieces, tags=(None, None)):
+            gather(0, b, ALL, tags[0])
+            gather(1, b, HEAD, tags[1])
+            gather(1, b, TAIL)
+            for tokens in pieces:
+                add_and_store(b, tokens)
+
+        scaled = tiles("scaled", 2, [P, TOKEN_TILES, 2 * P], F32)
+        turned = {}
+        summed = {}
+
+        def turn_gates(banks):
+            both = [(r, c) for r in range(2) for c in range(TOKEN_TILES)]
+            for n, number in enumerate(banks):
+                acc = bank(number)
+                for i, (r, c) in enumerate(both[4 * n : 4 * n + 4]):
+                    nc.tensor.transpose(acc[:, i * P : (i + 1) * P], gate_sb[r][:, c * P : (c + 1) * P], ident[:])
+                nc.scalar.copy(gate_col[:, 4 * n : 4 * n + 4], acc[:, 0:BANK:P])
+
+        def pick(h, banks):
+            first, last = TURNS[h]
+            width = (last - first) * P
+            plain = tile("plain%d" % h, [P, 2, 2, width], F32)
+            for r in range(2):
+                for v in range(2):
+                    picked = y[V0 + v][:].indirect(entries(pos_sb[r], first * P, last * P))
+                    nc.scalar.activation(plain[:, r, v, :], picked, COPY)
+                acc = bank(banks[r], 2 * width)
+                turned[r, h] = acc
+                for v in range(2):
+                    for i in range(last - first):
+                        at = (2 * i + v) * P
+                        nc.tensor.transpose(acc[:, at : at + P], plain[:, r, v, i * P : (i + 1) * P], ident[:])
+
+        def scale(h, number):
+            first, last = TURNS[h]
+            for r in range(2):
+                for c in range(first, last):
+                    column = gate_col[:, r * TOKEN_TILES + c : r * TOKEN_TILES + c + 1]
+                    at = 2 * (c - first) * P
+                    nc.scalar.activation(scaled[r][:, c, :], turned[r, h][:, at : at + 2 * P], COPY, scale=column)
+            acc = bank(number, 2 * (last - first) * P)
+            summed[h] = acc
+            for c in range(first, last):
+                for v in range(2):
+                    at = ((last - first) * v + c - first) * P
                     for r in range(2):
                         nc.tensor.matmul(
-                            acc[:, t : t + P],
-                            lhsT=gated[r][b][:, tokens.start + t : tokens.start + t + P],
+                            acc[:, at : at + P],
+                            lhsT=scaled[r][:, c, v * P : (v + 1) * P],
                             rhs=ident[:],
                             start=(r == 0),
                             stop=(r == 1),
                             is_transpose=True,
                         )
-                nc.scalar.copy(turned_sum[b][:, tokens], acc[:])
 
-        def turn_back(b, h, pair, parts=HALVES):
-            tokens = parts[h]
-            acc = bank(pair[h], tokens.stop - tokens.start)
-            for t in range(0, tokens.stop - tokens.start, P):
-                nc.tensor.transpose(acc[:, t : t + P], turned_sum[b][:, tokens.start + t : tokens.start + t + P], ident[:])
-            nc.scalar.copy(result[b][:, tokens], acc[:])
-
-        def add(b, tokens):
-            nc.vector.tensor_tensor(result[b][:, tokens], gated[0][b][:, tokens], gated[1][b][:, tokens], ADD)
-
-        def store(queue, b, tokens):
-            queue.dma_start(out[b * P : (b + 1) * P, tokens], result[b][:, tokens])
+        def finish(h):
+            tokens = slice(TURNS[h][0] * P, TURNS[h][1] * P)
+            nc.scalar.copy(result_v[:, :, tokens], summed[h][:].rearrange("p (v t) -> p v t", v=2))
+            rows = out[V0 * P : (V1 + 1) * P, tokens].rearrange("(v p) t -> p v t", p=P)
+            nc.sync.dma_start(rows, result_v[:, :, tokens])
 
         interleave_wk(0, nc.scalar.copy, 0, N // 2)
         interleave_wk(0, nc.scalar.copy, N // 2, N)
-        early = keep.tile([P, 3, N], U32, name="early", tag="token_words", align_bytes=64)
-        for e in range(3):
+        early = tile("early", [P, EARLY, N], U32, "token_words")
+        for e in range(EARLY):
             wk_w[e] = early[:, e, :]
-        quantise_wk(0, None)
+        quantise_wk(0)
         interleave_wk(1, nc.scalar.copy, 0, N // 2)
         interleave_wk(1, nc.scalar.copy, N // 2, N)
-        quantise_wk(1, None)
-        nc.gpsimd.tensor_scalar(wk_bf[2][:], wk_raw[2][:].rearrange("p j n -> p n j"), 1.0, 0.0, MULT, ADD)
-        quantise_wk(2, None)
-        project(Q0, (0, 1, 2, 3, 4, 5, 6), cuts=WORD_CUTS)
-        project(Q1, (7, 0, 1, 2, 3, 4))
-        gather_both(Q0)
-        gather_both(Q1)
-        interleave_wk(3, nc.scalar.copy, 0, N)
-        quantise_wk(3, "wk_w3")
-        project(V0, (1, 2, 3, 7,))
-        interleave_wk(4, nc.scalar.copy, 0, N)
-        quantise_wk(4, "wk_w4")
-        interleave_wk(5, nc.scalar.copy, 0, N)
-        quantise_wk(5, "wk_w5")
-        gather_both(V0)
-        add_turned(Q0, (1, 2,), tag="wk_raw5")
-        project(V1, (4, 5, 6,))
-        gated[0][V1] = keep.tile([P, T], F32, name="gated_late0V1", tag="wk_bf4", align_bytes=64)
-        gated[1][V1] = keep.tile([P, T], F32, name="gated_late1V1", tag="wk_bf5", align_bytes=64)
-        gather_both(V1)
-        turn_back(Q0, 0, (0, 1,))
-        turn_back(Q0, 1, (0, 1,))
-        store(nc.sync, Q0, ALL)
-        add_turned(Q1, (3, 7,), tag="wk_raw4")
-        project(K0, (4, 5, 6,))
-        gather(0, K0, ALL)
-        for tokens in THIRDS:
-            gather(1, K0, tokens)
-        add_turned(V0, (0, 1,))
-        turn_back(Q1, 0, (3, 7,))
-        turn_back(Q1, 1, (3, 7,))
-        store(nc.sync, Q1, ALL)
-        project(K1, (4, 5, 6,))
-        turn_back(V0, 0, (0, 1,))
-        turn_back(V0, 1, (0, 1,))
-        store(nc.sync, V0, ALL)
-        add_turned(V1, (3, 7,))
-        add_turned(K0, (4, 5, 6), (0, 1, 2), parts=THIRDS)
-        turn_back(V1, 0, (3, 7,))
-        store(nc.sync, V1, HALVES[0])
-        turn_back(V1, 1, (3, 7,))
-        store(nc.sync, V1, HALVES[1])
-        for h, tokens in enumerate(THIRDS):
-            turn_back(K0, h, (4, 5, 6), parts=THIRDS)
-            store(nc.sync, K0, tokens)
-        result[K1] = keep.tile([P, T], F32, name="last", tag="turned_sum%d" % K0, align_bytes=64)
-        gather(0, K1, ALL)
-        gather(1, K1, HEAD)
-        gather(1, K1, TAIL)
-        add(K1, THIRDS[0])
-        store(nc.sync, K1, THIRDS[0])
-        add(K1, THIRDS[1])
-        store(nc.sync, K1, THIRDS[1])
-        add(K1, THIRDS[2])
-        store(nc.sync, K1, THIRDS[2])
+        quantise_wk(1)
+        nc.gpsimd.tensor_scalar(wk_bf[2][:], wk_raw[2].rearrange("p j n -> p n j"), 1.0, 0.0, MULT, ADD)
+        quantise_wk(2)
+
+        interleave_wk(3, nc.vector.tensor_copy)
+        interleave_wk(4, nc.vector.tensor_copy)
+        quantise_wk(3)
+        interleave_wk(5, nc.vector.tensor_copy)
+        quantise_wk(4)
+        quantise_wk(5)
+
+        for e in range(E):
+            project(e, [(Q0, expert(e)), (Q1, expert(e))])
+        project_block(V0, (6, 7, 0))
+        project_block(V1, (1, 2, 3))
+        project_block(K0, (4, 5, 6))
+        project_block(K1, (7, 0, 1))
+        turn_gates((2, 3, 4))
+
+        combine(Q0, (HEAD, TAIL))
+        combine(Q1, (HEAD, TAIL))
+        combine(K0, (HEAD, TAIL))
+        result_v = tile("result_v", [P, 2, T], F32)
+        pick(0, (5, 6))
+        pick(1, (7, 0))
+        scale(0, 1)
+        pick(2, (2, 3))
+        finish(0)
+        scale(1, 4)
+        pick(3, (5, 6))
+        finish(1)
+        scale(2, 7)
+        scale(3, 0)
+        finish(2)
+        finish(3)
+        gather(0, K1, LAST[0])
+        gather(1, K1, LAST[0])
+        gather(0, K1, slice(LAST[1].start, T))
+        add_and_store(K1, LAST[0])
+        gather(1, K1, LAST[1])
+        gather(1, K1, LAST[2])
+        add_and_store(K1, LAST[1])
+        add_and_store(K1, LAST[2])

@@ -33,9 +33,10 @@ WORD_CUTS = (0, 256, 512, 1024, SLOTS)
 HEAD, TAIL, ALL = slice(0, 512), slice(512, T), slice(0, T)
 THIRDS = tuple(slice(t, t + T // 3) for t in range(0, T, T // 3))
 TOKEN_TILES = T // P
-TURNS = ((0, 2), (2, 4), (4, 5), (5, 6))
+TURNS = ((0, 2, 2), (2, 4, 2), (4, 5, 2), (5, 6, 1))
+REST = slice(T - P, T)
 LAST = (slice(0, 384), slice(384, 640), slice(640, T))
-EARLY = 3
+EARLY = 4
 
 
 def tile_moe_qkv_kernel(
@@ -64,8 +65,11 @@ def tile_moe_qkv_kernel(
         slot_scales = tile("slot_scales", [P, SLOTS], U8)
         wq_w, wv_w = tiles("fp4_words", 2, [P, E, 2 * N], U8)
         wq_s, wv_s = tiles("fp4_scales", 2, [P, E, N], U8)
-        wk_early = tiles("wk_early", E, [P, PACK, N], F32)
-        wk_raw = [t[:] for t in wk_early]
+        wk_early = tiles("wk_early", EARLY, [P, PACK, N], F32)
+        wk_late = tile("wk_late", [P, E - EARLY, PACK * N], F32)
+        wk_raw = [t[:] for t in wk_early] + [
+            wk_late[:, e, :].rearrange("p (j n) -> p j n", j=PACK) for e in range(E - EARLY)
+        ]
         wk_bf = tiles("wk_bf", E, [P, N, PACK], BF16)
         wk_s = tiles("wk_s", E, [P, N], U8)
         wk_w = {}
@@ -103,14 +107,13 @@ def tile_moe_qkv_kernel(
         load_fp4_words(wq_w, wq_words)
         nc.sync.dma_start(bias_q[:, :, 0:E], bias[0:N].rearrange("(b p) e -> p b e", p=P))
         nc.sync.dma_start(wk_early[2][:], wk_rows(2))
-        load_fp4_words(wv_w, wv_words)
         nc.sync.dma_start(wk_early[3][:], wk_rows(3))
+        load_fp4_words(wv_w, wv_words)
         load_fp4_scales(wv_s, wv_scales)
         nc.sync.dma_start(bias_kv[:, :, 0:E], bias[N : 3 * N].rearrange("(b p) e -> p b e", p=P))
-        nc.sync.dma_start(wk_early[4][:], wk_rows(4))
-        nc.sync.dma_start(wk_early[5][:], wk_rows(5))
         nc.sync.dma_start(gate_sb[0][:], gate[0])
         nc.sync.dma_start(pos_sb[0][:], pos1)
+        nc.sync.dma_start(wk_late[:], wk[EARLY:E].rearrange("e (p j) n -> p e (j n)", j=PACK))
         nc.sync.dma_start(gate_sb[1][:], gate[1])
         nc.sync.dma_start(pos_sb[1][:], pos2)
 
@@ -177,7 +180,6 @@ def tile_moe_qkv_kernel(
                 project(banks[pair % len(banks)], [(b, expert(2 * pair)), (b, expert(2 * pair + 1))])
 
         gated = {}
-        result = {}
 
         def gather(r, b, tokens, tag=None):
             if (r, b) not in gated:
@@ -186,10 +188,9 @@ def tile_moe_qkv_kernel(
             nc.vector.tensor_tensor(gated[r, b][:, tokens], picked, gate_sb[r][:, tokens], MULT)
 
         def add_and_store(b, tokens, tag=None):
-            if b not in result:
-                result[b] = tile("result%d" % b, [P, T], F32, tag)
-            nc.vector.tensor_tensor(result[b][:, tokens], gated[0, b][:, tokens], gated[1, b][:, tokens], ADD)
-            nc.sync.dma_start(out[b * P : (b + 1) * P, tokens], result[b][:, tokens])
+            result = tile("result%d_%d" % (b, tokens.start), [P, tokens.stop - tokens.start], F32, tag)
+            nc.vector.tensor_tensor(result[:], gated[0, b][:, tokens], gated[1, b][:, tokens], ADD)
+            nc.sync.dma_start(out[b * P : (b + 1) * P, tokens], result[:])
 
         def combine(b, pieces, tags=(None, None)):
             gather(0, b, ALL, tags[0])
@@ -198,7 +199,6 @@ def tile_moe_qkv_kernel(
             for tokens in pieces:
                 add_and_store(b, tokens)
 
-        scaled = tiles("scaled", 2, [P, TOKEN_TILES, 2 * P], F32)
         turned = {}
         summed = {}
 
@@ -211,47 +211,51 @@ def tile_moe_qkv_kernel(
                 nc.scalar.copy(gate_col[:, 4 * n : 4 * n + 4], acc[:, 0:BANK:P])
 
         def pick(h, banks):
-            first, last = TURNS[h]
+            first, last, count = TURNS[h]
             width = (last - first) * P
-            plain = tile("plain%d" % h, [P, 2, 2, width], F32)
+            plain = tile("plain%d" % h, [P, 2, count, width], F32)
             for r in range(2):
-                for v in range(2):
+                for v in range(count):
                     picked = y[V0 + v][:].indirect(entries(pos_sb[r], first * P, last * P))
                     nc.scalar.activation(plain[:, r, v, :], picked, COPY)
-                acc = bank(banks[r], 2 * width)
+                acc = bank(banks[r], count * width)
                 turned[r, h] = acc
-                for v in range(2):
+                for v in range(count):
                     for i in range(last - first):
-                        at = (2 * i + v) * P
+                        at = (count * i + v) * P
                         nc.tensor.transpose(acc[:, at : at + P], plain[:, r, v, i * P : (i + 1) * P], ident[:])
 
         def scale(h, number):
-            first, last = TURNS[h]
+            first, last, count = TURNS[h]
+            scaled = tile("scaled%d" % h, [P, 2, last - first, count * P], F32)
             for r in range(2):
                 for c in range(first, last):
                     column = gate_col[:, r * TOKEN_TILES + c : r * TOKEN_TILES + c + 1]
-                    at = 2 * (c - first) * P
-                    nc.scalar.activation(scaled[r][:, c, :], turned[r, h][:, at : at + 2 * P], COPY, scale=column)
-            acc = bank(number, 2 * (last - first) * P)
+                    at = count * (c - first) * P
+                    nc.scalar.activation(
+                        scaled[:, r, c - first, :], turned[r, h][:, at : at + count * P], COPY, scale=column
+                    )
+            acc = bank(number, count * (last - first) * P)
             summed[h] = acc
             for c in range(first, last):
-                for v in range(2):
+                for v in range(count):
                     at = ((last - first) * v + c - first) * P
                     for r in range(2):
                         nc.tensor.matmul(
                             acc[:, at : at + P],
-                            lhsT=scaled[r][:, c, v * P : (v + 1) * P],
+                            lhsT=scaled[:, r, c - first, v * P : (v + 1) * P],
                             rhs=ident[:],
                             start=(r == 0),
                             stop=(r == 1),
                             is_transpose=True,
                         )
 
-        def finish(h):
-            tokens = slice(TURNS[h][0] * P, TURNS[h][1] * P)
-            nc.scalar.copy(result_v[:, :, tokens], summed[h][:].rearrange("p (v t) -> p v t", v=2))
-            rows = out[V0 * P : (V1 + 1) * P, tokens].rearrange("(v p) t -> p v t", p=P)
-            nc.sync.dma_start(rows, result_v[:, :, tokens])
+        def finish(h, queue=nc.sync):
+            first, last, count = TURNS[h]
+            tokens = slice(first * P, last * P)
+            nc.scalar.copy(result_v[:, 0:count, tokens], summed[h][:].rearrange("p (v t) -> p v t", v=count))
+            rows = out[V0 * P : (V0 + count) * P, tokens].rearrange("(v p) t -> p v t", p=P)
+            queue.dma_start(rows, result_v[:, 0:count, tokens])
 
         interleave_wk(0, nc.scalar.copy, 0, N // 2)
         interleave_wk(0, nc.scalar.copy, N // 2, N)
@@ -262,45 +266,54 @@ def tile_moe_qkv_kernel(
         interleave_wk(1, nc.scalar.copy, 0, N // 2)
         interleave_wk(1, nc.scalar.copy, N // 2, N)
         quantise_wk(1)
-        nc.gpsimd.tensor_scalar(wk_bf[2][:], wk_raw[2].rearrange("p j n -> p n j"), 1.0, 0.0, MULT, ADD)
-        quantise_wk(2)
-
-        interleave_wk(3, nc.vector.tensor_copy)
-        interleave_wk(4, nc.vector.tensor_copy)
-        quantise_wk(3)
-        interleave_wk(5, nc.vector.tensor_copy)
-        quantise_wk(4)
-        quantise_wk(5)
+        for e in range(2, EARLY):
+            nc.gpsimd.tensor_scalar(wk_bf[e][:], wk_raw[e].rearrange("p j n -> p n j"), 1.0, 0.0, MULT, ADD)
+            quantise_wk(e)
 
         for e in range(E):
             project(e, [(Q0, expert(e)), (Q1, expert(e))])
         project_block(V0, (6, 7, 0))
         project_block(V1, (1, 2, 3))
-        project_block(K0, (4, 5, 6))
-        project_block(K1, (7, 0, 1))
-        turn_gates((2, 3, 4))
+        gather(0, Q0, ALL)
+        for e in range(EARLY, E):
+            interleave_wk(e, nc.vector.tensor_copy)
+        for e in range(EARLY, E):
+            quantise_wk(e)
+        project_block(K0, (1, 2, 3))
+        project_block(K1, (4, 5, 6))
+        turn_gates((7, 0, 1))
 
-        combine(Q0, (HEAD, TAIL))
-        combine(Q1, (HEAD, TAIL))
-        combine(K0, (HEAD, TAIL))
+        gather(1, Q0, HEAD)
+        gather(1, Q0, TAIL)
+        add_and_store(Q0, HEAD)
+        add_and_store(Q0, TAIL)
+        combine(Q1, (HEAD, TAIL), ("wk_bf4", None))
+        gather(0, V1, REST, "wk_bf5")
+        gather(1, V1, REST)
+        gather(0, K0, ALL)
+        add_and_store(V1, REST)
+        gather(1, K0, HEAD)
+        gather(1, K0, TAIL)
+        add_and_store(K0, HEAD)
+        add_and_store(K0, TAIL)
         result_v = tile("result_v", [P, 2, T], F32)
-        pick(0, (5, 6))
-        pick(1, (7, 0))
-        scale(0, 1)
-        pick(2, (2, 3))
+        pick(0, (2, 3))
+        pick(1, (4, 5))
+        scale(0, 6)
+        pick(2, (7, 0))
         finish(0)
-        scale(1, 4)
-        pick(3, (5, 6))
+        scale(1, 1)
+        pick(3, (2, 3))
         finish(1)
-        scale(2, 7)
-        scale(3, 0)
-        finish(2)
-        finish(3)
+        scale(2, 4)
+        scale(3, 5)
+        finish(2, nc.scalar)
+        finish(3, nc.scalar)
         gather(0, K1, LAST[0])
         gather(1, K1, LAST[0])
         gather(0, K1, slice(LAST[1].start, T))
-        add_and_store(K1, LAST[0])
+        add_and_store(K1, LAST[0], "scaled1")
         gather(1, K1, LAST[1])
         gather(1, K1, LAST[2])
-        add_and_store(K1, LAST[1])
-        add_and_store(K1, LAST[2])
+        add_and_store(K1, LAST[1], "scaled2")
+        add_and_store(K1, LAST[2], "scaled3")

@@ -279,9 +279,9 @@ def tile_moe_qkv_kernel(
             interleave_wk(e, nc.vector.tensor_copy)
         for e in range(EARLY, E):
             quantise_wk(e)
-        project_block(K0, (1, 2, 3))
-        project_block(K1, (4, 5, 6))
-        turn_gates((7, 0, 1))
+        project_block(K0, (6, 7, 0))
+        project_block(K1, (1, 2, 3))
+        turn_gates((4, 5, 6))
 
         gather(1, Q0, HEAD)
         gather(1, Q0, TAIL)
@@ -297,16 +297,16 @@ def tile_moe_qkv_kernel(
         add_and_store(K0, HEAD)
         add_and_store(K0, TAIL)
         result_v = tile("result_v", [P, 2, T], F32)
-        pick(0, (2, 3))
-        pick(1, (4, 5))
-        scale(0, 6)
-        pick(2, (7, 0))
+        pick(0, (7, 0))
+        pick(1, (1, 2))
+        scale(0, 3)
+        pick(2, (4, 5))
         finish(0)
-        scale(1, 1)
-        pick(3, (2, 3))
+        scale(1, 6)
+        pick(3, (7, 0))
         finish(1)
-        scale(2, 4)
-        scale(3, 5)
+        scale(2, 1)
+        scale(3, 2)
         finish(2, nc.scalar)
         finish(3, nc.scalar)
         gather(0, K1, LAST[0])

@@ -33,8 +33,7 @@ WORD_CUTS = (0, 256, 512, 1024, SLOTS)
 HEAD, TAIL, ALL = slice(0, 512), slice(512, T), slice(0, T)
 THIRDS = tuple(slice(t, t + T // 3) for t in range(0, T, T // 3))
 TOKEN_TILES = T // P
-TURNS = ((0, 2, 2), (2, 4, 2), (4, 5, 2), (5, 6, 1))
-REST = slice(T - P, T)
+TURNS = ((0, 2, 2), (2, 4, 2), (4, 5, 2), (5, 6, 2))
 LAST = (slice(0, 384), slice(384, 640), slice(640, T))
 EARLY = 4
 
@@ -187,10 +186,11 @@ def tile_moe_qkv_kernel(
             picked = y[b][:].indirect(entries(pos_sb[r], tokens.start, tokens.stop))
             nc.vector.tensor_tensor(gated[r, b][:, tokens], picked, gate_sb[r][:, tokens], MULT)
 
-        def add_and_store(b, tokens, tag=None):
-            result = tile("result%d_%d" % (b, tokens.start), [P, tokens.stop - tokens.start], F32, tag)
-            nc.vector.tensor_tensor(result[:], gated[0, b][:, tokens], gated[1, b][:, tokens], ADD)
-            nc.sync.dma_start(out[b * P : (b + 1) * P, tokens], result[:])
+        def add_and_store(b, tokens, tag=None, result=None):
+            if result is None:
+                result = tile("result%d_%d" % (b, tokens.start), [P, tokens.stop - tokens.start], F32, tag)[:]
+            nc.vector.tensor_tensor(result, gated[0, b][:, tokens], gated[1, b][:, tokens], ADD)
+            nc.sync.dma_start(out[b * P : (b + 1) * P, tokens], result)
 
         def combine(b, pieces, tags=(None, None)):
             gather(0, b, ALL, tags[0])
@@ -288,14 +288,7 @@ def tile_moe_qkv_kernel(
         add_and_store(Q0, HEAD)
         add_and_store(Q0, TAIL)
         combine(Q1, (HEAD, TAIL), ("wk_bf4", None))
-        gather(0, V1, REST, "wk_bf5")
-        gather(1, V1, REST)
-        gather(0, K0, ALL)
-        add_and_store(V1, REST)
-        gather(1, K0, HEAD)
-        gather(1, K0, TAIL)
-        add_and_store(K0, HEAD)
-        add_and_store(K0, TAIL)
+        combine(K0, (HEAD, TAIL))
         result_v = tile("result_v", [P, 2, T], F32)
         pick(0, (7, 0))
         pick(1, (1, 2))
@@ -315,5 +308,6 @@ def tile_moe_qkv_kernel(
         add_and_store(K1, LAST[0], "scaled1")
         gather(1, K1, LAST[1])
         gather(1, K1, LAST[2])
-        add_and_store(K1, LAST[1], "scaled2")
-        add_and_store(K1, LAST[2], "scaled3")
+        last = tile("last", [P, T - LAST[1].start], F32, "scaled2")
+        for tokens in LAST[1:]:
+            add_and_store(K1, tokens, None, last[:, tokens.start - LAST[1].start : tokens.stop - LAST[1].start])

@@ -74,11 +74,8 @@ def tile_moe_qkv_kernel(
         wk_w = {}
         y = tiles("y", BLOCKS, [P, SLOTS], F32)
         ident = tile("ident", [P, P], F32)
-        warm = tile("warm", [P, 8], F32)
 
         nc.gpsimd.memset(token_scales[:, 0:T].bitcast(I32), 0)
-        nc.vector.memset(warm[:, 0:1], 0.0)
-        nc.scalar.activation(warm[:, 4:5], warm[:, 0:1], IDENTITY)
         nc.vector.memset(token_scales[:, T:BYTE_WINDOW].bitcast(I32), 0)
         for scales in (wq_s, wv_s):
             nc.vector.memset(scales[:].rearrange("p e n -> p (e n)").bitcast(I32), 0)

@@ -25,11 +25,10 @@ PACK = 4
 PER_COLUMN = 16
 BLOCKS = 3 * N // P
 Q0, Q1, K0, K1, V0, V1 = range(BLOCKS)
-BIAS_PITCH = 8
 QUADRANT = 32
 BANK = 512
 BYTE_WINDOW = 2048
-WORD_CUTS = (0, 256, 512, 1024, SLOTS)
+WORD_CUTS = tuple(range(0, SLOTS + 1, C))
 HEAD, TAIL, ALL = slice(0, 512), slice(512, T), slice(0, T)
 THIRDS = tuple(slice(t, t + T // 3) for t in range(0, T, T // 3))
 TOKEN_TILES = T // P
@@ -56,8 +55,8 @@ def tile_moe_qkv_kernel(
         pos_sb = tiles("pos_sb", 2, [P, T // PER_COLUMN], U16)
         gate_sb = tiles("gate_sb", 2, [P, T], F32)
         gate_col = tile("gate_col", [P, 2 * TOKEN_TILES], F32)
-        bias_q = tile("bias_q", [P, 2, BIAS_PITCH], F32)
-        bias_kv = tile("bias_kv", [P, BLOCKS - 2, BIAS_PITCH], F32)
+        bias_rows = tile("bias_rows", [P, P, E], F32)
+        bias_col = tile("bias_col", [P, E, BLOCKS], F32)
         token_words = tile("token_words", [P, T], I32)
         token_scales = tile("token_scales", [P, BYTE_WINDOW], U8)
         slot_words = tile("slot_words", [P, SLOTS], U32)
@@ -76,9 +75,11 @@ def tile_moe_qkv_kernel(
         ident = tile("ident", [P, P], F32)
 
         nc.gpsimd.memset(token_scales[:, 0:T].bitcast(I32), 0)
+        nc.vector.memset(bias_rows[:], 0.0)
         nc.vector.memset(token_scales[:, T:BYTE_WINDOW].bitcast(I32), 0)
         for scales in (wq_s, wv_s):
             nc.vector.memset(scales[:].rearrange("p e n -> p (e n)").bitcast(I32), 0)
+        nc.gpsimd.dma_start(bias_rows[0:BLOCKS, :, :], bias.rearrange("(b p) e -> b p e", p=P))
         make_identity(nc, ident[:])
 
         def load_fp4_words(dst, src):
@@ -101,12 +102,10 @@ def tile_moe_qkv_kernel(
         nc.sync.dma_start(wk_early[1][:], wk_rows(1))
         load_fp4_scales(wq_s, wq_scales)
         load_fp4_words(wq_w, wq_words)
-        nc.sync.dma_start(bias_q[:, :, 0:E], bias[0:N].rearrange("(b p) e -> p b e", p=P))
         nc.sync.dma_start(wk_early[2][:], wk_rows(2))
         nc.sync.dma_start(wk_early[3][:], wk_rows(3))
         load_fp4_words(wv_w, wv_words)
         load_fp4_scales(wv_s, wv_scales)
-        nc.sync.dma_start(bias_kv[:, :, 0:E], bias[N : 3 * N].rearrange("(b p) e -> p b e", p=P))
         nc.sync.dma_start(gate_sb[0][:], gate[0])
         nc.sync.dma_start(pos_sb[0][:], pos1)
         nc.sync.dma_start(wk_late[:], wk[EARLY:E].rearrange("e (p j) n -> p e (j n)", j=PACK))
@@ -165,7 +164,7 @@ def tile_moe_qkv_kernel(
                 )
             for (b, slots), part in zip(pieces, parts):
                 e = slots.start // C
-                column = bias_q[:, b, e : e + 1] if b < 2 else bias_kv[:, b - 2, e : e + 1]
+                column = bias_col[:, e, b : b + 1]
                 nc.scalar.activation(y[b][:, slots], part, IDENTITY, bias=column)
 
         def expert(e):
@@ -198,6 +197,15 @@ def tile_moe_qkv_kernel(
 
         turned = {}
         summed = {}
+
+        def turn_bias(banks):
+            half = E // 2
+            for n, number in enumerate(banks):
+                acc = bank(number, half * P)
+                for i in range(half):
+                    nc.tensor.transpose(acc[:, i * P : (i + 1) * P], bias_rows[:, :, n * half + i], ident[:])
+                turned_rows = acc[:].rearrange("p (e k) -> p e k", k=P)[:, :, 0:BLOCKS]
+                nc.scalar.copy(bias_col[:, n * half : (n + 1) * half, :], turned_rows)
 
         def turn_gates(banks):
             both = [(r, c) for r in range(2) for c in range(TOKEN_TILES)]
@@ -263,6 +271,7 @@ def tile_moe_qkv_kernel(
         interleave_wk(1, nc.scalar.copy, 0, N // 2)
         interleave_wk(1, nc.scalar.copy, N // 2, N)
         quantise_wk(1)
+        turn_bias((6, 7))
         for e in range(2, EARLY):
             nc.gpsimd.tensor_scalar(wk_bf[e][:], wk_raw[e].rearrange("p j n -> p n j"), 1.0, 0.0, MULT, ADD)
             quantise_wk(e)

from contextlib import ExitStack

import concourse.mybir as mybir
from concourse.masks import make_identity

K, T, E, C, N = 512, 768, 6, 256, 256
SLOTS = E * C
FLOPS = 2 * K * SLOTS * 3 * N

F32 = mybir.dt.float32
BF16 = mybir.dt.bfloat16
I32 = mybir.dt.int32
U32 = mybir.dt.uint32
U16 = mybir.dt.uint16
U8 = mybir.dt.uint8
FP8X4 = mybir.dt.float8_e4m3fn_x4
FP4X4 = mybir.dt.float4_e2m1fn_x4
MULT = mybir.AluOpType.mult
ADD = mybir.AluOpType.add
IDENTITY = mybir.ActivationFunctionType.Identity
COPY = mybir.ActivationFunctionType.Copy

P = 128
PACK = 4
PER_COLUMN = 16
BLOCKS = 3 * N // P
Q0, Q1, K0, K1, V0, V1 = range(BLOCKS)
QUADRANT = 32
BANK = 512
BYTE_WINDOW = 2048
WORD_CUTS = tuple(range(0, SLOTS + 1, C))
HEAD, TAIL, ALL = slice(0, 512), slice(512, T), slice(0, T)
THIRDS = tuple(slice(t, t + T // 3) for t in range(0, T, T // 3))
TOKEN_TILES = T // P
TURNS = ((0, 2, 2), (2, 4, 2), (4, 5, 2), (5, 6, 2))
LAST = (slice(0, 384), slice(384, 640), slice(640, T))
EARLY = 4


def tile_moe_qkv_kernel(
    tc, x_words, x_scales, wq_words, wq_scales, wk, wv_words, wv_scales, bias, gate, offs, pos1, pos2, out
):
    nc = tc.nc
    with ExitStack() as ctx:
        keep = ctx.enter_context(tc.tile_pool(name="keep", bufs=1))
        psum = ctx.enter_context(tc.psum_pool(name="psum", bufs=1))

        def tile(name, shape, dtype, tag=None):
            return keep.tile(shape, dtype, name=name, tag=tag or name, align_bytes=64)

        def tiles(name, count, shape, dtype):
            return [tile("%s%d" % (name, i), shape, dtype) for i in range(count)]

        offs_sb = keep.tile([P, SLOTS // PER_COLUMN], U16, name="offs_sb")
        pos_sb = tiles("pos_sb", 2, [P, T // PER_COLUMN], U16)
        gate_sb = tiles("gate_sb", 2, [P, T], F32)
        gate_col = tile("gate_col", [P, 2 * TOKEN_TILES], F32)
        bias_rows = tile("bias_rows", [P, P, E], F32)
        bias_col = tile("bias_col", [P, E, BLOCKS], F32)
        token_words = tile("token_words", [P, T], I32)
        token_scales = tile("token_scales", [P, BYTE_WINDOW], U8)
        slot_words = tile("slot_words", [P, SLOTS], U32)
        slot_scales = tile("slot_scales", [P, SLOTS], U8)
        wq_w, wv_w = tiles("fp4_words", 2, [P, E, 2 * N], U8)
        wq_s, wv_s = tiles("fp4_scales", 2, [P, E, N], U8)
        wk_early = tiles("wk_early", EARLY, [P, PACK, N], F32)
        wk_late = tile("wk_late", [P, E - EARLY, PACK * N], F32)
        wk_raw = [t[:] for t in wk_early] + [
            wk_late[:, e, :].rearrange("p (j n) -> p j n", j=PACK) for e in range(E - EARLY)
        ]
        wk_bf = tiles("wk_bf", E, [P, N, PACK], BF16)
        wk_s = tiles("wk_s", E, [P, N], U8)
        wk_w = {}
        y = tiles("y", BLOCKS, [P, SLOTS], F32)
        ident = tile("ident", [P, P], F32)

        nc.gpsimd.memset(token_scales[:, 0:T].bitcast(I32), 0)
        nc.vector.memset(bias_rows[:], 0.0)
        nc.vector.memset(token_scales[:, T:BYTE_WINDOW].bitcast(I32), 0)
        for scales in (wq_s, wv_s):
            nc.vector.memset(scales[:].rearrange("p e n -> p (e n)").bitcast(I32), 0)
        nc.gpsimd.dma_start(bias_rows[0:BLOCKS, :, :], bias.rearrange("(b p) e -> b p e", p=P))
        make_identity(nc, ident[:])

        def load_fp4_words(dst, src):
            nc.sync.dma_start(dst[:].bitcast(I32), src.rearrange("e s p b -> p (e s) b").bitcast(I32))

        def load_fp4_scales(dst, src):
            for i in range(4):
                rows = src[:, 0, i::4, :].rearrange("e q n -> q e n")
                nc.sync.dma_start(dst[i:P:QUADRANT, :, :].bitcast(I32), rows.bitcast(I32))

        def wk_rows(e):
            return wk[e].rearrange("(p j) n -> p j n", j=PACK)

        nc.sync.dma_start(offs_sb[:], offs)
        nc.sync.dma_start(wk_early[0][:, 0:2, :], wk_rows(0)[:, 0:2, :])
        for i in range(4):
            nc.sync.dma_start(token_scales[i:P:QUADRANT, 0:T].bitcast(I32), x_scales[0, i::4, :].bitcast(I32))
        nc.sync.dma_start(wk_early[0][:, 2:4, :], wk_rows(0)[:, 2:4, :])
        nc.sync.dma_start(token_words[:], x_words[0].rearrange("p t d -> p (t d)").bitcast(I32))
        nc.sync.dma_start(wk_early[1][:], wk_rows(1))
        load_fp4_scales(wq_s, wq_scales)
        load_fp4_words(wq_w, wq_words)
        nc.sync.dma_start(wk_early[2][:], wk_rows(2))
        nc.sync.dma_start(wk_early[3][:], wk_rows(3))
        load_fp4_words(wv_w, wv_words)
        load_fp4_scales(wv_s, wv_scales)
        nc.sync.dma_start(gate_sb[0][:], gate[0])
        nc.sync.dma_start(pos_sb[0][:], pos1)
        nc.sync.dma_start(wk_late[:], wk[EARLY:E].rearrange("e (p j) n -> p e (j n)", j=PACK))
        nc.sync.dma_start(gate_sb[1][:], gate[1])
        nc.sync.dma_start(pos_sb[1][:], pos2)

        def entries(list_sb, first, last):
            return list_sb[:, first // PER_COLUMN : last // PER_COLUMN]

        nc.vector.tensor_copy(slot_scales[:], token_scales[:].indirect(offs_sb[:]))
        for first, last in zip(WORD_CUTS[:-1], WORD_CUTS[1:]):
            picked = token_words[:].bitcast(U32).indirect(entries(offs_sb, first, last))
            nc.vector.tensor_copy(slot_words[:, first:last], picked)

        taken = []

        def bank(number, width=BANK):
            taken.append(width)
            return psum.tile([P, width], F32, name="acc%d" % len(taken), tag="bank%d" % number)

        def interleave_wk(e, copy, first=0, last=N):
            src = wk_raw[e].rearrange("p j (c i) -> p c j i", i=4)
            dst = wk_bf[e][:].rearrange("p (c i) j -> p c j i", i=4)
            copy(dst[:, first // 4 : last // 4, :, :], src[:, first // 4 : last // 4, :, :])

        def quantise_wk(e):
            if e not in wk_w:
                wk_w[e] = tile("wk_w%d" % e, [P, N], U32)[:]
            nc.vector.quantize_mx(
                out=wk_w[e].bitcast(FP8X4), scales=wk_s[e][:], in_=wk_bf[e][:].rearrange("p n j -> p (n j)")
            )

        def project(number, pieces):
            acc = bank(number, sum(s.stop - s.start for b, s in pieces))
            at = 0
            parts = []
            for b, slots in pieces:
                part = acc[:, at : at + slots.stop - slots.start]
                at = at + slots.stop - slots.start
                parts.append(part)
                e = slots.start // C
                cols = slice(b % 2 * P, (b % 2 + 1) * P)
                if b in (K0, K1):
                    w, w_scale = wk_w[e][:, cols].bitcast(FP8X4), wk_s[e][:, cols]
                else:
                    words, scales = (wq_w, wq_s) if b in (Q0, Q1) else (wv_w, wv_s)
                    w, w_scale = words[:, e, 2 * cols.start : 2 * cols.stop].bitcast(FP4X4), scales[:, e, cols]
                nc.tensor.matmul_mx(
                    out=part,
                    lhsT=w,
                    lhsT_scale=w_scale,
                    rhs=slot_words[:, slots].bitcast(FP8X4),
                    rhs_scale=slot_scales[:, slots],
                    start=True,
                    stop=True,
                )
            for (b, slots), part in zip(pieces, parts):
                e = slots.start // C
                column = bias_col[:, e, b : b + 1]
                nc.scalar.activation(y[b][:, slots], part, IDENTITY, bias=column)

        def expert(e):
            return slice(e * C, (e + 1) * C)

        def project_block(b, banks):
            for pair in range(E // 2):
                project(banks[pair % len(banks)], [(b, expert(2 * pair)), (b, expert(2 * pair + 1))])

        gated = {}

        def gather(r, b, tokens, tag=None):
            if (r, b) not in gated:
                gated[r, b] = tile("gated%d_%d" % (r, b), [P, T], F32, tag)
            picked = y[b][:].indirect(entries(pos_sb[r], tokens.start, tokens.stop))
            nc.vector.tensor_tensor(gated[r, b][:, tokens], picked, gate_sb[r][:, tokens], MULT)

        def add_and_store(b, tokens, tag=None, result=None):
            if result is None:
                result = tile("result%d_%d" % (b, tokens.start), [P, tokens.stop - tokens.start], F32, tag)[:]
            nc.vector.tensor_tensor(result, gated[0, b][:, tokens], gated[1, b][:, tokens], ADD)
            nc.sync.dma_start(out[b * P : (b + 1) * P, tokens], result)

        def combine(b, pieces, tags=(None, None)):
            gather(0, b, ALL, tags[0])
            gather(1, b, HEAD, tags[1])
            gather(1, b, TAIL)
            for tokens in pieces:
                add_and_store(b, tokens)

        turned = {}
        summed = {}

        def turn_bias(banks):
            half = E // 2
            for n, number in enumerate(banks):
                acc = bank(number, half * P)
                for i in range(half):
                    nc.tensor.transpose(acc[:, i * P : (i + 1) * P], bias_rows[:, :, n * half + i], ident[:])
                turned_rows = acc[:].rearrange("p (e k) -> p e k", k=P)[:, :, 0:BLOCKS]
                nc.scalar.copy(bias_col[:, n * half : (n + 1) * half, :], turned_rows)

        def turn_gates(banks):
            both = [(r, c) for r in range(2) for c in range(TOKEN_TILES)]
            for n, number in enumerate(banks):
                acc = bank(number)
                for i, (r, c) in enumerate(both[4 * n : 4 * n + 4]):
                    nc.tensor.transpose(acc[:, i * P : (i + 1) * P], gate_sb[r][:, c * P : (c + 1) * P], ident[:])
                nc.scalar.copy(gate_col[:, 4 * n : 4 * n + 4], acc[:, 0:BANK:P])

        def pick(h, banks):
            first, last, count = TURNS[h]
            width = (last - first) * P
            plain = tile("plain%d" % h, [P, 2, count, width], F32)
            for r in range(2):
                for v in range(count):
                    picked = y[V0 + v][:].indirect(entries(pos_sb[r], first * P, last * P))
                    nc.scalar.activation(plain[:, r, v, :], picked, COPY)
                acc = bank(banks[r], count * width)
                turned[r, h] = acc
                for v in range(count):
                    for i in range(last - first):
                        at = (count * i + v) * P
                        nc.tensor.transpose(acc[:, at : at + P], plain[:, r, v, i * P : (i + 1) * P], ident[:])

        def scale(h, number):
            first, last, count = TURNS[h]
            scaled = tile("scaled%d" % h, [P, 2, last - first, count * P], F32)
            for r in range(2):
                for c in range(first, last):
                    column = gate_col[:, r * TOKEN_TILES + c : r * TOKEN_TILES + c + 1]
                    at = count * (c - first) * P
                    nc.scalar.activation(
                        scaled[:, r, c - first, :], turned[r, h][:, at : at + count * P], COPY, scale=column
                    )
            acc = bank(number, count * (last - first) * P)
            summed[h] = acc
            for c in range(first, last):
                for v in range(count):
                    at = ((last - first) * v + c - first) * P
                    for r in range(2):
                        nc.tensor.matmul(
                            acc[:, at : at + P],
                            lhsT=scaled[:, r, c - first, v * P : (v + 1) * P],
                            rhs=ident[:],
                            start=(r == 0),
                            stop=(r == 1),
                            is_transpose=True,
                        )

        def finish(h, queue=nc.sync):
            first, last, count = TURNS[h]
            tokens = slice(first * P, last * P)
            nc.scalar.copy(result_v[:, 0:count, tokens], summed[h][:].rearrange("p (v t) -> p v t", v=count))
            rows = out[V0 * P : (V0 + count) * P, tokens].rearrange("(v p) t -> p v t", p=P)
            queue.dma_start(rows, result_v[:, 0:count, tokens])

        interleave_wk(0, nc.scalar.copy, 0, N // 2)
        interleave_wk(0, nc.scalar.copy, N // 2, N)
        early = tile("early", [P, EARLY, N], U32, "token_words")
        for e in range(EARLY):
            wk_w[e] = early[:, e, :]
        quantise_wk(0)
        interleave_wk(1, nc.scalar.copy, 0, N // 2)
        interleave_wk(1, nc.scalar.copy, N // 2, N)
        quantise_wk(1)
        turn_bias((6, 7))
        for e in range(2, EARLY):
            nc.gpsimd.tensor_scalar(wk_bf[e][:], wk_raw[e].rearrange("p j n -> p n j"), 1.0, 0.0, MULT, ADD)
            quantise_wk(e)

        for e in range(E):
            project(e, [(Q0, expert(e)), (Q1, expert(e))])
        project_block(V0, (6, 7, 0))
        project_block(V1, (1, 2, 3))
        gather(0, Q0, ALL)
        for e in range(EARLY, E):
            interleave_wk(e, nc.vector.tensor_copy)
        for e in range(EARLY, E):
            quantise_wk(e)
        project_block(K0, (6, 7, 0))
        project_block(K1, (1, 2, 3))
        turn_gates((4, 5, 6))

        gather(1, Q0, HEAD)
        gather(1, Q0, TAIL)
        add_and_store(Q0, HEAD)
        add_and_store(Q0, TAIL)
        combine(Q1, (HEAD, TAIL), ("wk_bf4", None))
        combine(K0, (HEAD, TAIL))
        result_v = tile("result_v", [P, 2, T], F32)
        pick(0, (7, 0))
        pick(1, (1, 2))
        scale(0, 3)
        pick(2, (4, 5))
        finish(0)
        scale(1, 6)
        pick(3, (7, 0))
        finish(1)
        scale(2, 1)
        scale(3, 2)
        finish(2, nc.scalar)
        finish(3, nc.scalar)
        gather(0, K1, LAST[0])
        gather(1, K1, LAST[0])
        gather(0, K1, slice(LAST[1].start, T))
        add_and_store(K1, LAST[0], "scaled1")
        gather(1, K1, LAST[1])
        gather(1, K1, LAST[2])
        last = tile("last", [P, T - LAST[1].start], F32, "scaled2")
        for tokens in LAST[1:]:
            add_and_store(K1, tokens, None, last[:, tokens.start - LAST[1].start : tokens.stop - LAST[1].start])
